import numpy as np
import ml_dtypes


def mxq(x, axis, fmt="e4m3"):
    dtype, down = {"e4m3": (ml_dtypes.float8_e4m3fn, 7), "e5m2": (ml_dtypes.float8_e5m2, 14)}[fmt]
    v = np.moveaxis(np.asarray(x, np.float32).astype(ml_dtypes.bfloat16).astype(np.float64), axis, -1)
    blocks = v.reshape(v.shape[:-1] + (-1, 32))
    amax = np.abs(blocks).max(-1, keepdims=True)
    byte = np.maximum(np.where(amax > 0, np.frexp(amax)[1] - 1 + 127, 0) - down, 1)
    scale = np.exp2(byte - 127.0)
    codes = (blocks / scale).astype(np.float32).astype(dtype).astype(np.float64)
    return np.moveaxis((codes * scale).reshape(v.shape), -1, axis)


WIDE = False


def mx_kscale(k):
    if not WIDE:
        return np.ones(k)
    levels = np.array([10, -10, 5, -5, 0])
    if k % 512:
        return np.exp2(np.random.permutation(np.resize(levels, k // 32))).repeat(32)
    a = np.empty((k // 512, 16))
    for p in range(k // 512):
        a[p, :8] = np.random.permutation(np.resize(levels, 8))
        for g in range(8):
            far = levels[np.abs(levels - a[p, g]) >= 10]
            a[p, g + 8] = far[np.random.randint(len(far))]
    return np.exp2(a.ravel()).repeat(32)


def f64(x):
    return np.asarray(x).astype(np.float64)


def striped(idx):
    return np.tile(np.asarray(idx).reshape(-1, 16).T, (8, 1)).astype(np.uint16)


def unstriped(offs):
    return offs[:16].T.reshape(-1).astype(np.int64)


E2M1 = np.array([0.0, 0.5, 1.0, 1.5, 2.0, 3.0, 4.0, 6.0, -0.0, -0.5, -1.0, -1.5, -2.0, -3.0, -4.0, -6.0])


def pack_weight(w, fmt):
    k, n = w.shape
    w = f64(np.asarray(w, np.float32).astype(ml_dtypes.bfloat16)).reshape(k // 32, 32, n)
    amax = np.abs(w).max(1)
    if fmt == "e4m3":
        byte = np.frexp(amax)[1] - 1 + 127 - 7
    else:
        mant, ex = np.frexp(amax / 6.0)
        byte = np.where(mant > 0.5, ex, ex - 1) + 127
    byte = np.clip(np.where(amax > 0, byte, 1), 1, 254)
    scaled = (w * np.exp2(127.0 - byte)[:, None, :]).reshape(k, n).astype(np.float32)
    by_word = np.ascontiguousarray(scaled.reshape(k // 512, 128, 4, n).transpose(0, 1, 3, 2))
    if fmt == "e4m3":
        words = by_word.astype(ml_dtypes.float8_e4m3fn).view(np.uint8)
    else:
        c = by_word.astype(ml_dtypes.float4_e2m1fn).view(np.uint8) & 0xF
        words = (c[..., 0::2] | (c[..., 1::2] << 4)).reshape(k // 512, 128, 2 * n)
    return np.ascontiguousarray(words), np.ascontiguousarray(byte.astype(np.uint8).reshape(k // 512, 16, n))


def unpack_weight(words, scales, fmt):
    g, _, n = scales.shape
    words = np.ascontiguousarray(words).reshape(g, 128, n, -1)
    if fmt == "e4m3":
        vals = words.view(ml_dtypes.float8_e4m3fn).astype(np.float64)
    else:
        nib = np.empty((g, 128, n, 4), np.uint8)
        nib[..., 0::2] = words & 0xF
        nib[..., 1::2] = words >> 4
        vals = E2M1[nib]
    vals = vals * np.repeat(np.exp2(scales.astype(np.float64) - 127.0), 8, axis=1)[..., None]
    return vals.transpose(0, 1, 3, 2).reshape(g * 512, n)


D, K, T, I, U, Q = 512, 512, 4096, 1024, 512, 128


def setup_inputs():
    n = np.random.standard_normal
    idx = np.random.permutation(T)[:I]
    idx2 = np.random.randint(0, U, I)
    fd = mx_kscale(D)
    fk = mx_kscale(K)
    tailp = pack_weight(n((K, T)) / fk[:, None], "e4m3")
    return {
        "hid": (n((D, Q)) * 1.0 / np.sqrt(D) * fd[:, None]).astype(np.float32),
        "head": (n((D, U)) / fd[:, None]).astype(np.float32),
        "tl": (np.random.uniform(0.5, 1.5, (Q, U))).astype(np.float32),
        "htail": (n((K, Q)) * 1.0 / np.sqrt(K) * fk[:, None]).astype(np.float32),
        "tail_words": tailp[0],
        "tail_scales": tailp[1],
        "offs": striped(idx),
        "offs2": striped(idx2),
    }


def reference(hid, head, tl, htail, tail_words, tail_scales, offs, offs2):
    idx = unstriped(offs)
    idx2 = unstriped(offs2)
    tailu = unpack_weight(tail_words, tail_scales, "e4m3")
    hidq = mxq(f64(hid), 0, "e4m3")
    headq = mxq(f64(head), 0, "e4m3")
    a = hidq.T @ headq
    p = np.exp(a)
    b = a - np.log(np.sum(p, axis=1, keepdims=True)) - f64(tl)
    htailq = mxq(f64(htail), 0, "e4m3")
    tailidxg = tailu[:, idx]
    r = htailq.T @ tailidxg
    y = b[:, idx2] + r
    return y

@@ -1,0 +1,167 @@
+from contextlib import ExitStack
+
+import concourse.mybir as mybir
+
+D, K, T, I, U, Q = 512, 512, 4096, 1024, 512, 128
+FLOPS = 2 * Q * D * U + 2 * Q * K * I
+
+F32 = mybir.dt.float32
+BF16 = mybir.dt.bfloat16
+I32 = mybir.dt.int32
+U32 = mybir.dt.uint32
+U16 = mybir.dt.uint16
+U8 = mybir.dt.uint8
+FP8X4 = mybir.dt.float8_e4m3fn_x4
+ALU = mybir.AluOpType
+ACT = mybir.ActivationFunctionType
+AXIS = mybir.AxisListType
+
+P = 128
+PACK = 4
+HALF_U = U // 2
+HALF_I = I // 2
+SPARE = 32
+SCALE_ROW = P - 16
+SCALAR_U = 96
+
+
+def interleave(copy, grouped, raw):
+    copy(
+        grouped.rearrange("p (c i) t -> p c t i", i=4),
+        raw.rearrange("p t (c i) -> p c t i", i=4),
+    )
+
+
+def quantise(nc, codes, scales, grouped):
+    nc.vector.quantize_mx(
+        out=codes.bitcast(FP8X4),
+        scales=scales,
+        in_=grouped.rearrange("p w t -> p (w t)"),
+    )
+
+
+def tile_attend_adaptivesoftmax_kernel(tc, hid, head, tl, htail, tail_words, tail_scales, offs, offs2, out):
+    nc = tc.nc
+    with ExitStack() as ctx:
+        lists = ctx.enter_context(tc.tile_pool(name="lists", bufs=1))
+        sb = ctx.enter_context(tc.tile_pool(name="sb", bufs=1))
+        ps = ctx.enter_context(tc.psum_pool(name="ps", bufs=1))
+
+        word_list = lists.tile([P, I // 16], U16, name="word_list")
+        cluster_list = lists.tile([P, I // 16], U16, name="cluster_list")
+
+        scale_pool = sb.tile([P, T], U8, name="scale_pool", tag="scales_then_b", align_bytes=64)
+        nc.vector.memset(scale_pool[:].bitcast(I32)[:SCALE_ROW, :], 0)
+
+        tail_plane = sb.tile([P, I], U8, name="tail_plane", align_bytes=64)
+        nc.vector.memset(tail_plane[:].bitcast(I32), 0)
+
+        hid_raw = sb.tile([P, PACK, Q], F32, name="hid_raw")
+        nc.sync.dma_start(out=hid_raw[:], in_=hid.rearrange("(p t) q -> p t q", t=PACK))
+        head_raw = [sb.tile([P, PACK, HALF_U], F32, name="head_raw%d" % h) for h in range(2)]
+        for h in range(2):
+            nc.sync.dma_start(
+                out=head_raw[h][:],
+                in_=head[:, h * HALF_U : (h + 1) * HALF_U].rearrange("(p t) u -> p t u", t=PACK),
+            )
+        htail_raw = sb.tile([P, PACK, Q], F32, name="htail_raw")
+        nc.sync.dma_start(out=htail_raw[:], in_=htail.rearrange("(p t) q -> p t q", t=PACK))
+        tl_sb = sb.tile([P, U], F32, name="tl_sb", tag="tl_then_scales", align_bytes=64)
+        nc.sync.dma_start(out=tl_sb[:], in_=tl)
+        nc.sync.dma_start(word_list[:], offs)
+        nc.sync.dma_start(out=scale_pool[:].bitcast(I32)[SCALE_ROW:, :], in_=tail_scales[0].bitcast(I32))
+        nc.sync.dma_start(cluster_list[:], offs2)
+        word_pool = sb.tile([P, T], U32, name="word_pool", align_bytes=64)
+        nc.sync.dma_start(
+            out=word_pool[:].bitcast(I32),
+            in_=tail_words[0].rearrange("p n t -> p (n t)").bitcast(I32),
+        )
+
+        hid_grouped = sb.tile([P, Q, PACK], BF16, name="hid_grouped", align_bytes=64)
+        hid_codes = sb.tile([P, Q], U32, name="hid_codes", align_bytes=64)
+        hid_scales = sb.tile([P, Q], U8, name="hid_scales", align_bytes=64)
+        interleave(nc.scalar.copy, hid_grouped[:], hid_raw[:])
+        quantise(nc, hid_codes[:], hid_scales[:], hid_grouped[:])
+
+        head_codes = sb.tile([P, U], U32, name="head_codes", align_bytes=64)
+        head_scales = sb.tile([P, U], U8, name="head_scales", align_bytes=64)
+        head_grouped = [sb.tile([P, HALF_U, PACK], BF16, name="head_grouped%d" % h, align_bytes=64) for h in range(2)]
+        a = ps.tile([P, U], F32, name="a")
+        interleave(nc.vector.tensor_copy, head_grouped[0][:], head_raw[0][:])
+        interleave(nc.scalar.copy, head_grouped[1][:, :SCALAR_U, :], head_raw[1][:, :, :SCALAR_U])
+        for h in range(2):
+            cols = slice(h * HALF_U, (h + 1) * HALF_U)
+            if h == 1:
+                interleave(nc.vector.tensor_copy, head_grouped[1][:, SCALAR_U:, :], head_raw[1][:, :, SCALAR_U:])
+            quantise(nc, head_codes[:, cols], head_scales[:, cols], head_grouped[h][:])
+            nc.tensor.matmul_mx(
+                out=a[:, cols],
+                lhsT=hid_codes[:].bitcast(FP8X4),
+                lhsT_scale=hid_scales[:],
+                rhs=head_codes[:, cols].bitcast(FP8X4),
+                rhs_scale=head_scales[:, cols],
+                start=True,
+                stop=True,
+            )
+
+        htail_grouped = sb.tile([P, Q, PACK], BF16, name="htail_grouped", align_bytes=64)
+        htail_codes = sb.tile([P, Q], U32, name="htail_codes", align_bytes=64)
+        htail_scales = sb.tile([P, Q], U8, name="htail_scales", align_bytes=64)
+        interleave(nc.scalar.copy, htail_grouped[:], htail_raw[:])
+
+        neg_max = sb.tile([P, 1], F32, name="neg_max")
+        nc.vector.tensor_reduce(neg_max[:], a[:], AXIS.X, ALU.max, negate=True)
+        p = sb.tile([P, U], F32, name="p")
+        row_sum = sb.tile([P, 1], F32, name="row_sum")
+        nc.scalar.activation(p[:], a[:], ACT.Exp, bias=neg_max[:], accum_out=row_sum[:])
+        shifted = sb.tile([P, U], F32, name="shifted")
+        nc.vector.scalar_tensor_tensor(shifted[:], a[:], neg_max[:], tl_sb[:], ALU.add, ALU.subtract)
+        log_sum = sb.tile([P, 1], F32, name="log_sum")
+        nc.scalar.activation(log_sum[:], row_sum[:], ACT.Ln)
+
+        quantise(nc, htail_codes[:], htail_scales[:], htail_grouped[:])
+        listed_scales = sb.tile([P, I], U8, name="listed_scales", tag="tl_then_scales", align_bytes=64)
+        nc.vector.tensor_copy(listed_scales[:], scale_pool[:].indirect(word_list[:]))
+        for row in range(4):
+            nc.scalar.dma_start(
+                out=tail_plane[:].bitcast(I32)[row:P:32, :],
+                in_=listed_scales[:].bitcast(I32)[SCALE_ROW + row : P : 4, :],
+            )
+
+        b = sb.tile([P, U + SPARE], F32, name="b", tag="scales_then_b", align_bytes=64)
+        nc.vector.memset(b[:, U:], 0.0)
+        nc.vector.tensor_scalar(b[:, :U], shifted[:], log_sum[:], None, ALU.subtract)
+
+        halves = [slice(h * HALF_I // 16, (h + 1) * HALF_I // 16) for h in range(2)]
+        listed_b = sb.tile([P, HALF_I], F32, name="listed_b")
+        nc.vector.tensor_copy(listed_b[:], b[:].indirect(cluster_list[:, halves[1]]))
+
+        listed_words = [sb.tile([P, HALF_I], U32, name="listed_words%d" % h, align_bytes=64) for h in range(2)]
+        for h in range(2):
+            nc.vector.tensor_copy(listed_words[h][:], word_pool[:].indirect(word_list[:, halves[h]]))
+
+        def tail_logits(bank, first, width):
+            h, start = divmod(first, HALF_I)
+            nc.tensor.matmul_mx(
+                out=bank[:, :width],
+                lhsT=htail_codes[:].bitcast(FP8X4),
+                lhsT_scale=htail_scales[:],
+                rhs=listed_words[h][:, start : start + width].bitcast(FP8X4),
+                rhs_scale=tail_plane[:, first : first + width],
+                start=True,
+                stop=True,
+            )
+
+        r_sb = sb.tile([P, HALF_I], F32, name="r_sb")
+        for quarter in range(2):
+            bank = ps.tile([P, HALF_I // 2], F32, name="r%d" % quarter)
+            tail_logits(bank, quarter * HALF_I // 2, HALF_I // 2)
+            nc.scalar.copy(r_sb[:, quarter * HALF_I // 2 : (quarter + 1) * HALF_I // 2], bank[:])
+        r_last = ps.tile([P, HALF_I], F32, name="r_last")
+        tail_logits(r_last, HALF_I, HALF_I)
+
+        y = [sb.tile([P, HALF_I], F32, name="y%d" % h) for h in range(2)]
+        nc.vector.tensor_tensor(y[0][:], b[:].indirect(cluster_list[:, halves[0]]), r_sb[:], ALU.add)
+        nc.sync.dma_start(out=out[:, :HALF_I], in_=y[0][:])
+        nc.vector.tensor_tensor(y[1][:], r_last[:], listed_b[:], ALU.add)
+        nc.scalar.dma_start(out=out[:, HALF_I:], in_=y[1][:])

@@ -22,7 +22,9 @@ HALF_U = U // 2
 HALF_I = I // 2
 SPARE = 32
 SCALE_ROW = P - 16
-SCALAR_U = 96
+SCALAR_U = (192, 160)
+ROOT = 16
+TERMS = 28
 
 
 def interleave(copy, grouped, raw):
@@ -50,15 +52,14 @@ def tile_attend_adaptivesoftmax_kernel(tc, hid, head, tl, htail, tail_words, tai
         word_list = lists.tile([P, I // 16], U16, name="word_list")
         cluster_list = lists.tile([P, I // 16], U16, name="cluster_list")
 
-        scale_pool = sb.tile([P, T], U8, name="scale_pool", tag="scales_then_b", align_bytes=64)
+        scale_pool = sb.tile([P, T], U8, name="scale_pool", align_bytes=64)
         nc.vector.memset(scale_pool[:].bitcast(I32)[:SCALE_ROW, :], 0)
 
-        tail_plane = sb.tile([P, I], U8, name="tail_plane", align_bytes=64)
-        nc.vector.memset(tail_plane[:].bitcast(I32), 0)
-
+        nc.sync.dma_start(word_list[:], offs)
+        nc.sync.dma_start(out=scale_pool[:].bitcast(I32)[SCALE_ROW:, :], in_=tail_scales[0].bitcast(I32))
         hid_raw = sb.tile([P, PACK, Q], F32, name="hid_raw")
         nc.sync.dma_start(out=hid_raw[:], in_=hid.rearrange("(p t) q -> p t q", t=PACK))
-        head_raw = [sb.tile([P, PACK, HALF_U], F32, name="head_raw%d" % h) for h in range(2)]
+        head_raw = [sb.tile([P, PACK, HALF_U], F32, name="head_raw%d" % h, tag="head_raw%d" % h, align_bytes=64) for h in range(2)]
         for h in range(2):
             nc.sync.dma_start(
                 out=head_raw[h][:],
@@ -66,16 +67,32 @@ def tile_attend_adaptivesoftmax_kernel(tc, hid, head, tl, htail, tail_words, tai
             )
         htail_raw = sb.tile([P, PACK, Q], F32, name="htail_raw")
         nc.sync.dma_start(out=htail_raw[:], in_=htail.rearrange("(p t) q -> p t q", t=PACK))
-        tl_sb = sb.tile([P, U], F32, name="tl_sb", tag="tl_then_scales", align_bytes=64)
+        tl_sb = sb.tile([P, U], F32, name="tl_sb")
         nc.sync.dma_start(out=tl_sb[:], in_=tl)
-        nc.sync.dma_start(word_list[:], offs)
-        nc.sync.dma_start(out=scale_pool[:].bitcast(I32)[SCALE_ROW:, :], in_=tail_scales[0].bitcast(I32))
         nc.sync.dma_start(cluster_list[:], offs2)
         word_pool = sb.tile([P, T], U32, name="word_pool", align_bytes=64)
         nc.sync.dma_start(
             out=word_pool[:].bitcast(I32),
             in_=tail_words[0].rearrange("p n t -> p (n t)").bitcast(I32),
         )
+
+        b = sb.tile([P, U + SPARE], F32, name="b")
+        nc.vector.memset(b[:, U:], 0.0)
+
+        powers = sb.tile([P, TERMS], I32, name="powers")
+        nc.gpsimd.iota(powers[:], [[-1, TERMS]], base=TERMS, channel_multiplier=0)
+        fractions = sb.tile([P, TERMS], F32, name="fractions")
+        nc.vector.tensor_scalar(fractions[:], powers[:], 1.0 / ROOT, None, ALU.mult)
+        coefficients = sb.tile([P, TERMS + 1], F32, name="coefficients")
+        nc.vector.reciprocal(coefficients[:, :TERMS], fractions[:])
+        nc.vector.memset(coefficients[:, TERMS:], 0.0)
+        minus_ones = sb.tile([P, TERMS + 1], F32, name="minus_ones")
+        nc.vector.memset(minus_ones[:], -1.0)
+        exponent = sb.tile([P, 1], F32, name="exponent")
+        nc.gpsimd.memset(exponent[:], 1.0 / ROOT)
+
+        listed_scales = sb.tile([P, I], U8, name="listed_scales", align_bytes=64)
+        nc.vector.tensor_copy(listed_scales[:], scale_pool[:].indirect(word_list[:]))
 
         hid_grouped = sb.tile([P, Q, PACK], BF16, name="hid_grouped", align_bytes=64)
         hid_codes = sb.tile([P, Q], U32, name="hid_codes", align_bytes=64)
@@ -87,12 +104,11 @@ def tile_attend_adaptivesoftmax_kernel(tc, hid, head, tl, htail, tail_words, tai
         head_scales = sb.tile([P, U], U8, name="head_scales", align_bytes=64)
         head_grouped = [sb.tile([P, HALF_U, PACK], BF16, name="head_grouped%d" % h, align_bytes=64) for h in range(2)]
         a = ps.tile([P, U], F32, name="a")
-        interleave(nc.vector.tensor_copy, head_grouped[0][:], head_raw[0][:])
-        interleave(nc.scalar.copy, head_grouped[1][:, :SCALAR_U, :], head_raw[1][:, :, :SCALAR_U])
         for h in range(2):
             cols = slice(h * HALF_U, (h + 1) * HALF_U)
-            if h == 1:
-                interleave(nc.vector.tensor_copy, head_grouped[1][:, SCALAR_U:, :], head_raw[1][:, :, SCALAR_U:])
+            cut = SCALAR_U[h]
+            interleave(nc.scalar.copy, head_grouped[h][:, :cut, :], head_raw[h][:, :, :cut])
+            interleave(nc.vector.tensor_copy, head_grouped[h][:, cut:, :], head_raw[h][:, :, cut:])
             quantise(nc, head_codes[:, cols], head_scales[:, cols], head_grouped[h][:])
             nc.tensor.matmul_mx(
                 out=a[:, cols],
@@ -109,34 +125,37 @@ def tile_attend_adaptivesoftmax_kernel(tc, hid, head, tl, htail, tail_words, tai
         htail_scales = sb.tile([P, Q], U8, name="htail_scales", align_bytes=64)
         interleave(nc.scalar.copy, htail_grouped[:], htail_raw[:])
 
-        neg_max = sb.tile([P, 1], F32, name="neg_max")
-        nc.vector.tensor_reduce(neg_max[:], a[:], AXIS.X, ALU.max, negate=True)
-        p = sb.tile([P, U], F32, name="p")
-        row_sum = sb.tile([P, 1], F32, name="row_sum")
-        nc.scalar.activation(p[:], a[:], ACT.Exp, bias=neg_max[:], accum_out=row_sum[:])
-        shifted = sb.tile([P, U], F32, name="shifted")
-        nc.vector.scalar_tensor_tensor(shifted[:], a[:], neg_max[:], tl_sb[:], ALU.add, ALU.subtract)
-        log_sum = sb.tile([P, 1], F32, name="log_sum")
-        nc.scalar.activation(log_sum[:], row_sum[:], ACT.Ln)
-
-        quantise(nc, htail_codes[:], htail_scales[:], htail_grouped[:])
-        listed_scales = sb.tile([P, I], U8, name="listed_scales", tag="tl_then_scales", align_bytes=64)
-        nc.vector.tensor_copy(listed_scales[:], scale_pool[:].indirect(word_list[:]))
+        tail_plane = sb.tile([P, I], U8, name="tail_plane", tag="head_raw1", align_bytes=64)
+        nc.vector.memset(tail_plane[:].bitcast(I32), 0)
         for row in range(4):
             nc.scalar.dma_start(
                 out=tail_plane[:].bitcast(I32)[row:P:32, :],
                 in_=listed_scales[:].bitcast(I32)[SCALE_ROW + row : P : 4, :],
             )
 
-        b = sb.tile([P, U + SPARE], F32, name="b", tag="scales_then_b", align_bytes=64)
-        nc.vector.memset(b[:, U:], 0.0)
-        nc.vector.tensor_scalar(b[:, :U], shifted[:], log_sum[:], None, ALU.subtract)
+        neg_a = sb.tile([P, U], F32, name="neg_a")
+        neg_max = sb.tile([P, 1], F32, name="neg_max")
+        nc.vector.tensor_scalar(neg_a[:], a[:], -1.0, None, ALU.mult, ALU.min, accum_out=neg_max[:])
+        p = sb.tile([P, U], F32, name="p")
+        row_sum = sb.tile([P, 1], F32, name="row_sum")
+        nc.scalar.activation(p[:], a[:], ACT.Exp, bias=neg_max[:], accum_out=row_sum[:])
+        a_less_tl = sb.tile([P, U], F32, name="a_less_tl", tag="listed_words0", align_bytes=64)
+        nc.vector.scalar_tensor_tensor(a_less_tl[:], neg_a[:], -1.0, tl_sb[:], ALU.mult, ALU.subtract)
+        quantise(nc, htail_codes[:], htail_scales[:], htail_grouped[:])
+
+        root = sb.tile([P, 1], F32, name="root")
+        nc.gpsimd.tensor_tensor(root[:], row_sum[:], exponent[:], ALU.pow)
+        gap = sb.tile([P, TERMS + 1], F32, name="gap")
+        nc.vector.tensor_scalar(gap[:], minus_ones[:], root[:], 1.0, ALU.mult, ALU.add)
+        series = sb.tile([P, TERMS + 1], F32, name="series")
+        nc.vector.tensor_tensor_scan(series[:], gap[:], coefficients[:], 0.0, ALU.mult, ALU.add)
+        nc.vector.tensor_scalar(b[:, :U], a_less_tl[:], neg_max[:], series[:, TERMS:], ALU.add, ALU.add)
 
         halves = [slice(h * HALF_I // 16, (h + 1) * HALF_I // 16) for h in range(2)]
         listed_b = sb.tile([P, HALF_I], F32, name="listed_b")
         nc.vector.tensor_copy(listed_b[:], b[:].indirect(cluster_list[:, halves[1]]))
 
-        listed_words = [sb.tile([P, HALF_I], U32, name="listed_words%d" % h, align_bytes=64) for h in range(2)]
+        listed_words = [sb.tile([P, HALF_I], U32, name="listed_words%d" % h, tag="listed_words%d" % h, align_bytes=64) for h in range(2)]
         for h in range(2):
             nc.vector.tensor_copy(listed_words[h][:], word_pool[:].indirect(word_list[:, halves[h]]))
 
@@ -160,8 +179,11 @@ def tile_attend_adaptivesoftmax_kernel(tc, hid, head, tl, htail, tail_words, tai
         r_last = ps.tile([P, HALF_I], F32, name="r_last")
         tail_logits(r_last, HALF_I, HALF_I)
 
-        y = [sb.tile([P, HALF_I], F32, name="y%d" % h) for h in range(2)]
-        nc.vector.tensor_tensor(y[0][:], b[:].indirect(cluster_list[:, halves[0]]), r_sb[:], ALU.add)
-        nc.sync.dma_start(out=out[:, :HALF_I], in_=y[0][:])
-        nc.vector.tensor_tensor(y[1][:], r_last[:], listed_b[:], ALU.add)
-        nc.scalar.dma_start(out=out[:, HALF_I:], in_=y[1][:])
+        y = sb.tile([P, HALF_I], F32, name="y")
+        nc.vector.tensor_tensor(y[:], b[:].indirect(cluster_list[:, halves[0]]), r_sb[:], ALU.add)
+        nc.sync.dma_start(out=out[:, :HALF_I], in_=y[:])
+        for quarter, queue in enumerate((nc.scalar, nc.sync)):
+            cols = slice(quarter * HALF_I // 2, (quarter + 1) * HALF_I // 2)
+            y_last = sb.tile([P, HALF_I // 2], F32, name="y_last%d" % quarter)
+            nc.vector.tensor_tensor(y_last[:], r_last[:, cols], listed_b[:, cols], ALU.add)
+            queue.dma_start(out=out[:, HALF_I + cols.start : HALF_I + cols.stop], in_=y_last[:])

@@ -18,13 +18,11 @@ AXIS = mybir.AxisListType
 
 P = 128
 PACK = 4
-HALF_U = U // 2
 HALF_I = I // 2
+QUARTER_I = I // 4
 SPARE = 32
 SCALE_ROW = P - 16
-SCALAR_U = (192, 160)
-ROOT = 16
-TERMS = 28
+SCALAR_U = 208
 
 
 def interleave(copy, grouped, raw):
@@ -54,42 +52,25 @@ def tile_attend_adaptivesoftmax_kernel(tc, hid, head, tl, htail, tail_words, tai
 
         scale_pool = sb.tile([P, T], U8, name="scale_pool", align_bytes=64)
         nc.vector.memset(scale_pool[:].bitcast(I32)[:SCALE_ROW, :], 0)
+        b = sb.tile([P, U + SPARE], F32, name="b")
+        nc.vector.memset(b[:, U:], 0.0)
 
-        nc.sync.dma_start(word_list[:], offs)
-        nc.sync.dma_start(out=scale_pool[:].bitcast(I32)[SCALE_ROW:, :], in_=tail_scales[0].bitcast(I32))
         hid_raw = sb.tile([P, PACK, Q], F32, name="hid_raw")
         nc.sync.dma_start(out=hid_raw[:], in_=hid.rearrange("(p t) q -> p t q", t=PACK))
-        head_raw = [sb.tile([P, PACK, HALF_U], F32, name="head_raw%d" % h, tag="head_raw%d" % h, align_bytes=64) for h in range(2)]
-        for h in range(2):
-            nc.sync.dma_start(
-                out=head_raw[h][:],
-                in_=head[:, h * HALF_U : (h + 1) * HALF_U].rearrange("(p t) u -> p t u", t=PACK),
-            )
+        nc.sync.dma_start(word_list[:], offs)
+        nc.sync.dma_start(out=scale_pool[:].bitcast(I32)[SCALE_ROW:, :], in_=tail_scales[0].bitcast(I32))
+        head_raw = sb.tile([P, PACK, U], F32, name="head_raw", tag="head_then_plane", align_bytes=64)
+        nc.sync.dma_start(out=head_raw[:], in_=head.rearrange("(p t) u -> p t u", t=PACK))
+        nc.sync.dma_start(cluster_list[:], offs2)
         htail_raw = sb.tile([P, PACK, Q], F32, name="htail_raw")
         nc.sync.dma_start(out=htail_raw[:], in_=htail.rearrange("(p t) q -> p t q", t=PACK))
         tl_sb = sb.tile([P, U], F32, name="tl_sb")
         nc.sync.dma_start(out=tl_sb[:], in_=tl)
-        nc.sync.dma_start(cluster_list[:], offs2)
         word_pool = sb.tile([P, T], U32, name="word_pool", align_bytes=64)
         nc.sync.dma_start(
             out=word_pool[:].bitcast(I32),
             in_=tail_words[0].rearrange("p n t -> p (n t)").bitcast(I32),
         )
-
-        b = sb.tile([P, U + SPARE], F32, name="b")
-        nc.vector.memset(b[:, U:], 0.0)
-
-        powers = sb.tile([P, TERMS], I32, name="powers")
-        nc.gpsimd.iota(powers[:], [[-1, TERMS]], base=TERMS, channel_multiplier=0)
-        fractions = sb.tile([P, TERMS], F32, name="fractions")
-        nc.vector.tensor_scalar(fractions[:], powers[:], 1.0 / ROOT, None, ALU.mult)
-        coefficients = sb.tile([P, TERMS + 1], F32, name="coefficients")
-        nc.vector.reciprocal(coefficients[:, :TERMS], fractions[:])
-        nc.vector.memset(coefficients[:, TERMS:], 0.0)
-        minus_ones = sb.tile([P, TERMS + 1], F32, name="minus_ones")
-        nc.vector.memset(minus_ones[:], -1.0)
-        exponent = sb.tile([P, 1], F32, name="exponent")
-        nc.gpsimd.memset(exponent[:], 1.0 / ROOT)
 
         listed_scales = sb.tile([P, I], U8, name="listed_scales", align_bytes=64)
         nc.vector.tensor_copy(listed_scales[:], scale_pool[:].indirect(word_list[:]))
@@ -100,32 +81,29 @@ def tile_attend_adaptivesoftmax_kernel(tc, hid, head, tl, htail, tail_words, tai
         interleave(nc.scalar.copy, hid_grouped[:], hid_raw[:])
         quantise(nc, hid_codes[:], hid_scales[:], hid_grouped[:])
 
+        head_grouped = sb.tile([P, U, PACK], BF16, name="head_grouped", align_bytes=64)
         head_codes = sb.tile([P, U], U32, name="head_codes", align_bytes=64)
         head_scales = sb.tile([P, U], U8, name="head_scales", align_bytes=64)
-        head_grouped = [sb.tile([P, HALF_U, PACK], BF16, name="head_grouped%d" % h, align_bytes=64) for h in range(2)]
+        interleave(nc.scalar.copy, head_grouped[:, :SCALAR_U, :], head_raw[:, :, :SCALAR_U])
+        interleave(nc.vector.tensor_copy, head_grouped[:, SCALAR_U:, :], head_raw[:, :, SCALAR_U:])
+        quantise(nc, head_codes[:], head_scales[:], head_grouped[:])
         a = ps.tile([P, U], F32, name="a")
-        for h in range(2):
-            cols = slice(h * HALF_U, (h + 1) * HALF_U)
-            cut = SCALAR_U[h]
-            interleave(nc.scalar.copy, head_grouped[h][:, :cut, :], head_raw[h][:, :, :cut])
-            interleave(nc.vector.tensor_copy, head_grouped[h][:, cut:, :], head_raw[h][:, :, cut:])
-            quantise(nc, head_codes[:, cols], head_scales[:, cols], head_grouped[h][:])
-            nc.tensor.matmul_mx(
-                out=a[:, cols],
-                lhsT=hid_codes[:].bitcast(FP8X4),
-                lhsT_scale=hid_scales[:],
-                rhs=head_codes[:, cols].bitcast(FP8X4),
-                rhs_scale=head_scales[:, cols],
-                start=True,
-                stop=True,
-            )
+        nc.tensor.matmul_mx(
+            out=a[:],
+            lhsT=hid_codes[:].bitcast(FP8X4),
+            lhsT_scale=hid_scales[:],
+            rhs=head_codes[:].bitcast(FP8X4),
+            rhs_scale=head_scales[:],
+            start=True,
+            stop=True,
+        )
 
         htail_grouped = sb.tile([P, Q, PACK], BF16, name="htail_grouped", align_bytes=64)
         htail_codes = sb.tile([P, Q], U32, name="htail_codes", align_bytes=64)
         htail_scales = sb.tile([P, Q], U8, name="htail_scales", align_bytes=64)
         interleave(nc.scalar.copy, htail_grouped[:], htail_raw[:])
 
-        tail_plane = sb.tile([P, I], U8, name="tail_plane", tag="head_raw1", align_bytes=64)
+        tail_plane = sb.tile([P, I], U8, name="tail_plane", tag="head_then_plane", align_bytes=64)
         nc.vector.memset(tail_plane[:].bitcast(I32), 0)
         for row in range(4):
             nc.scalar.dma_start(
@@ -139,51 +117,38 @@ def tile_attend_adaptivesoftmax_kernel(tc, hid, head, tl, htail, tail_words, tai
         p = sb.tile([P, U], F32, name="p")
         row_sum = sb.tile([P, 1], F32, name="row_sum")
         nc.scalar.activation(p[:], a[:], ACT.Exp, bias=neg_max[:], accum_out=row_sum[:])
-        a_less_tl = sb.tile([P, U], F32, name="a_less_tl", tag="listed_words0", align_bytes=64)
+        a_less_tl = sb.tile([P, U], F32, name="a_less_tl")
         nc.vector.scalar_tensor_tensor(a_less_tl[:], neg_a[:], -1.0, tl_sb[:], ALU.mult, ALU.subtract)
         quantise(nc, htail_codes[:], htail_scales[:], htail_grouped[:])
 
-        root = sb.tile([P, 1], F32, name="root")
-        nc.gpsimd.tensor_tensor(root[:], row_sum[:], exponent[:], ALU.pow)
-        gap = sb.tile([P, TERMS + 1], F32, name="gap")
-        nc.vector.tensor_scalar(gap[:], minus_ones[:], root[:], 1.0, ALU.mult, ALU.add)
-        series = sb.tile([P, TERMS + 1], F32, name="series")
-        nc.vector.tensor_tensor_scan(series[:], gap[:], coefficients[:], 0.0, ALU.mult, ALU.add)
-        nc.vector.tensor_scalar(b[:, :U], a_less_tl[:], neg_max[:], series[:, TERMS:], ALU.add, ALU.add)
+        log_sum = sb.tile([P, 1], F32, name="log_sum")
+        nc.scalar.activation(log_sum[:], row_sum[:], ACT.Ln)
+        neg_lse = sb.tile([P, 1], F32, name="neg_lse")
+        nc.scalar.activation(neg_lse[:], log_sum[:], ACT.Identity, bias=neg_max[:], scale=-1.0)
+        nc.scalar.activation(b[:, :U], a_less_tl[:], ACT.Identity, bias=neg_lse[:])
 
-        halves = [slice(h * HALF_I // 16, (h + 1) * HALF_I // 16) for h in range(2)]
-        listed_b = sb.tile([P, HALF_I], F32, name="listed_b")
-        nc.vector.tensor_copy(listed_b[:], b[:].indirect(cluster_list[:, halves[1]]))
-
-        listed_words = [sb.tile([P, HALF_I], U32, name="listed_words%d" % h, tag="listed_words%d" % h, align_bytes=64) for h in range(2)]
+        listed_words = [sb.tile([P, HALF_I], U32, name="listed_words%d" % h, align_bytes=64) for h in range(2)]
         for h in range(2):
-            nc.vector.tensor_copy(listed_words[h][:], word_pool[:].indirect(word_list[:, halves[h]]))
+            entries = slice(h * HALF_I // 16, (h + 1) * HALF_I // 16)
+            nc.vector.tensor_copy(listed_words[h][:], word_pool[:].indirect(word_list[:, entries]))
 
-        def tail_logits(bank, first, width):
+        r_sb = sb.tile([P, I], F32, name="r_sb")
+        for first in range(0, I, QUARTER_I):
             h, start = divmod(first, HALF_I)
+            bank = ps.tile([P, QUARTER_I], F32, name="r%d" % first)
             nc.tensor.matmul_mx(
-                out=bank[:, :width],
+                out=bank[:],
                 lhsT=htail_codes[:].bitcast(FP8X4),
                 lhsT_scale=htail_scales[:],
-                rhs=listed_words[h][:, start : start + width].bitcast(FP8X4),
-                rhs_scale=tail_plane[:, first : first + width],
+                rhs=listed_words[h][:, start : start + QUARTER_I].bitcast(FP8X4),
+                rhs_scale=tail_plane[:, first : first + QUARTER_I],
                 start=True,
                 stop=True,
             )
+            nc.scalar.copy(r_sb[:, first : first + QUARTER_I], bank[:])
 
-        r_sb = sb.tile([P, HALF_I], F32, name="r_sb")
-        for quarter in range(2):
-            bank = ps.tile([P, HALF_I // 2], F32, name="r%d" % quarter)
-            tail_logits(bank, quarter * HALF_I // 2, HALF_I // 2)
-            nc.scalar.copy(r_sb[:, quarter * HALF_I // 2 : (quarter + 1) * HALF_I // 2], bank[:])
-        r_last = ps.tile([P, HALF_I], F32, name="r_last")
-        tail_logits(r_last, HALF_I, HALF_I)
-
-        y = sb.tile([P, HALF_I], F32, name="y")
-        nc.vector.tensor_tensor(y[:], b[:].indirect(cluster_list[:, halves[0]]), r_sb[:], ALU.add)
-        nc.sync.dma_start(out=out[:, :HALF_I], in_=y[:])
-        for quarter, queue in enumerate((nc.scalar, nc.sync)):
-            cols = slice(quarter * HALF_I // 2, (quarter + 1) * HALF_I // 2)
-            y_last = sb.tile([P, HALF_I // 2], F32, name="y_last%d" % quarter)
-            nc.vector.tensor_tensor(y_last[:], r_last[:, cols], listed_b[:, cols], ALU.add)
-            queue.dma_start(out=out[:, HALF_I + cols.start : HALF_I + cols.stop], in_=y_last[:])
+        for first, last, queue in ((0, HALF_I, nc.sync), (HALF_I, I - QUARTER_I, nc.scalar), (I - QUARTER_I, I, nc.sync)):
+            y = sb.tile([P, last - first], F32, name="y%d" % first)
+            listed_b = b[:].indirect(cluster_list[:, first // 16 : last // 16])
+            nc.vector.tensor_tensor(y[:], listed_b, r_sb[:, first:last], ALU.add)
+            queue.dma_start(out=out[:, first:last], in_=y[:])

@@ -64,13 +64,13 @@ def tile_attend_adaptivesoftmax_kernel(tc, hid, head, tl, htail, tail_words, tai
         nc.sync.dma_start(cluster_list[:], offs2)
         htail_raw = sb.tile([P, PACK, Q], F32, name="htail_raw")
         nc.sync.dma_start(out=htail_raw[:], in_=htail.rearrange("(p t) q -> p t q", t=PACK))
-        tl_sb = sb.tile([P, U], F32, name="tl_sb")
-        nc.sync.dma_start(out=tl_sb[:], in_=tl)
         word_pool = sb.tile([P, T], U32, name="word_pool", align_bytes=64)
         nc.sync.dma_start(
             out=word_pool[:].bitcast(I32),
             in_=tail_words[0].rearrange("p n t -> p (n t)").bitcast(I32),
         )
+        tl_sb = sb.tile([P, U], F32, name="tl_sb")
+        nc.sync.dma_start(out=tl_sb[:], in_=tl)
 
         listed_scales = sb.tile([P, I], U8, name="listed_scales", align_bytes=64)
         nc.vector.tensor_copy(listed_scales[:], scale_pool[:].indirect(word_list[:]))
@@ -86,17 +86,18 @@ def tile_attend_adaptivesoftmax_kernel(tc, hid, head, tl, htail, tail_words, tai
         head_scales = sb.tile([P, U], U8, name="head_scales", align_bytes=64)
         interleave(nc.scalar.copy, head_grouped[:, :SCALAR_U, :], head_raw[:, :, :SCALAR_U])
         interleave(nc.vector.tensor_copy, head_grouped[:, SCALAR_U:, :], head_raw[:, :, SCALAR_U:])
-        quantise(nc, head_codes[:], head_scales[:], head_grouped[:])
         a = ps.tile([P, U], F32, name="a")
-        nc.tensor.matmul_mx(
-            out=a[:],
-            lhsT=hid_codes[:].bitcast(FP8X4),
-            lhsT_scale=hid_scales[:],
-            rhs=head_codes[:].bitcast(FP8X4),
-            rhs_scale=head_scales[:],
-            start=True,
-            stop=True,
-        )
+        for cols in (slice(U // 2, U), slice(0, U // 2)):
+            quantise(nc, head_codes[:, cols], head_scales[:, cols], head_grouped[:, cols, :])
+            nc.tensor.matmul_mx(
+                out=a[:, cols],
+                lhsT=hid_codes[:].bitcast(FP8X4),
+                lhsT_scale=hid_scales[:],
+                rhs=head_codes[:, cols].bitcast(FP8X4),
+                rhs_scale=head_scales[:, cols],
+                start=True,
+                stop=True,
+            )
 
         htail_grouped = sb.tile([P, Q, PACK], BF16, name="htail_grouped", align_bytes=64)
         htail_codes = sb.tile([P, Q], U32, name="htail_codes", align_bytes=64)
@@ -117,22 +118,25 @@ def tile_attend_adaptivesoftmax_kernel(tc, hid, head, tl, htail, tail_words, tai
         p = sb.tile([P, U], F32, name="p")
         row_sum = sb.tile([P, 1], F32, name="row_sum")
         nc.scalar.activation(p[:], a[:], ACT.Exp, bias=neg_max[:], accum_out=row_sum[:])
-        a_less_tl = sb.tile([P, U], F32, name="a_less_tl")
-        nc.vector.scalar_tensor_tensor(a_less_tl[:], neg_a[:], -1.0, tl_sb[:], ALU.mult, ALU.subtract)
+        tl_less_a = sb.tile([P, U], F32, name="tl_less_a", tag="r_second", align_bytes=64)
+        nc.gpsimd.tensor_tensor(tl_less_a[:], neg_a[:], tl_sb[:], ALU.add)
         quantise(nc, htail_codes[:], htail_scales[:], htail_grouped[:])
 
         log_sum = sb.tile([P, 1], F32, name="log_sum")
         nc.scalar.activation(log_sum[:], row_sum[:], ACT.Ln)
-        neg_lse = sb.tile([P, 1], F32, name="neg_lse")
+        neg_lse = sb.tile([P, 1], F32, name="neg_lse", tag="r_quarter1", align_bytes=64)
         nc.scalar.activation(neg_lse[:], log_sum[:], ACT.Identity, bias=neg_max[:], scale=-1.0)
-        nc.scalar.activation(b[:, :U], a_less_tl[:], ACT.Identity, bias=neg_lse[:])
+        nc.scalar.activation(b[:, :U], tl_less_a[:], ACT.Identity, bias=neg_lse[:], scale=-1.0)
 
         listed_words = [sb.tile([P, HALF_I], U32, name="listed_words%d" % h, align_bytes=64) for h in range(2)]
         for h in range(2):
             entries = slice(h * HALF_I // 16, (h + 1) * HALF_I // 16)
             nc.vector.tensor_copy(listed_words[h][:], word_pool[:].indirect(word_list[:, entries]))
 
-        r_sb = sb.tile([P, I], F32, name="r_sb")
+        r_quarter0 = sb.tile([P, QUARTER_I], F32, name="r_quarter0")
+        r_quarter1 = sb.tile([P, QUARTER_I], F32, name="r_quarter1", tag="r_quarter1", align_bytes=64)
+        r_second = sb.tile([P, HALF_I], F32, name="r_second", tag="r_second", align_bytes=64)
+        r_sb = [r_quarter0[:], r_quarter1[:], r_second[:, :QUARTER_I], r_second[:, QUARTER_I:]]
         for first in range(0, I, QUARTER_I):
             h, start = divmod(first, HALF_I)
             bank = ps.tile([P, QUARTER_I], F32, name="r%d" % first)
@@ -145,10 +149,11 @@ def tile_attend_adaptivesoftmax_kernel(tc, hid, head, tl, htail, tail_words, tai
                 start=True,
                 stop=True,
             )
-            nc.scalar.copy(r_sb[:, first : first + QUARTER_I], bank[:])
+            nc.scalar.copy(r_sb[first // QUARTER_I], bank[:])
 
-        for first, last, queue in ((0, HALF_I, nc.sync), (HALF_I, I - QUARTER_I, nc.scalar), (I - QUARTER_I, I, nc.sync)):
-            y = sb.tile([P, last - first], F32, name="y%d" % first)
+        for quarter, queue in enumerate((nc.sync, nc.sync, nc.scalar, nc.sync)):
+            first, last = quarter * QUARTER_I, (quarter + 1) * QUARTER_I
+            y = sb.tile([P, QUARTER_I], F32, name="y%d" % quarter)
             listed_b = b[:].indirect(cluster_list[:, first // 16 : last // 16])
-            nc.vector.tensor_tensor(y[:], listed_b, r_sb[:, first:last], ALU.add)
+            nc.vector.tensor_tensor(y[:], listed_b, r_sb[quarter], ALU.add)
             queue.dma_start(out=out[:, first:last], in_=y[:])

@@ -1,3 +1,4 @@
+import math
 from contextlib import ExitStack
 
 import concourse.mybir as mybir
@@ -20,9 +21,10 @@ P = 128
 PACK = 4
 HALF_I = I // 2
 QUARTER_I = I // 4
-SPARE = 32
 SCALE_ROW = P - 16
 SCALAR_U = 208
+LN_PER_BIT = math.log(2.0) / 2**23
+GUESS_SHIFT = 88.0
 
 
 def interleave(copy, grouped, raw):
@@ -52,16 +54,14 @@ def tile_attend_adaptivesoftmax_kernel(tc, hid, head, tl, htail, tail_words, tai
 
         scale_pool = sb.tile([P, T], U8, name="scale_pool", align_bytes=64)
         nc.vector.memset(scale_pool[:].bitcast(I32)[:SCALE_ROW, :], 0)
-        b = sb.tile([P, U + SPARE], F32, name="b")
-        nc.vector.memset(b[:, U:], 0.0)
+        b = sb.tile([P, U], F32, name="b")
 
-        hid_raw = sb.tile([P, PACK, Q], F32, name="hid_raw")
-        nc.sync.dma_start(out=hid_raw[:], in_=hid.rearrange("(p t) q -> p t q", t=PACK))
         nc.sync.dma_start(word_list[:], offs)
         nc.sync.dma_start(out=scale_pool[:].bitcast(I32)[SCALE_ROW:, :], in_=tail_scales[0].bitcast(I32))
+        hid_raw = sb.tile([P, PACK, Q], F32, name="hid_raw")
+        nc.sync.dma_start(out=hid_raw[:], in_=hid.rearrange("(p t) q -> p t q", t=PACK))
         head_raw = sb.tile([P, PACK, U], F32, name="head_raw", tag="head_then_plane", align_bytes=64)
         nc.sync.dma_start(out=head_raw[:], in_=head.rearrange("(p t) u -> p t u", t=PACK))
-        nc.sync.dma_start(cluster_list[:], offs2)
         htail_raw = sb.tile([P, PACK, Q], F32, name="htail_raw")
         nc.sync.dma_start(out=htail_raw[:], in_=htail.rearrange("(p t) q -> p t q", t=PACK))
         word_pool = sb.tile([P, T], U32, name="word_pool", align_bytes=64)
@@ -71,6 +71,7 @@ def tile_attend_adaptivesoftmax_kernel(tc, hid, head, tl, htail, tail_words, tai
         )
         tl_sb = sb.tile([P, U], F32, name="tl_sb")
         nc.sync.dma_start(out=tl_sb[:], in_=tl)
+        nc.sync.dma_start(cluster_list[:], offs2)
 
         listed_scales = sb.tile([P, I], U8, name="listed_scales", align_bytes=64)
         nc.vector.tensor_copy(listed_scales[:], scale_pool[:].indirect(word_list[:]))
@@ -112,31 +113,36 @@ def tile_attend_adaptivesoftmax_kernel(tc, hid, head, tl, htail, tail_words, tai
                 in_=listed_scales[:].bitcast(I32)[SCALE_ROW + row : P : 4, :],
             )
 
-        neg_a = sb.tile([P, U], F32, name="neg_a")
         neg_max = sb.tile([P, 1], F32, name="neg_max")
-        nc.vector.tensor_scalar(neg_a[:], a[:], -1.0, None, ALU.mult, ALU.min, accum_out=neg_max[:])
+        nc.vector.tensor_reduce(neg_max[:], a[:], AXIS.X, ALU.max, negate=True)
         p = sb.tile([P, U], F32, name="p")
         row_sum = sb.tile([P, 1], F32, name="row_sum")
         nc.scalar.activation(p[:], a[:], ACT.Exp, bias=neg_max[:], accum_out=row_sum[:])
-        tl_less_a = sb.tile([P, U], F32, name="tl_less_a", tag="r_second", align_bytes=64)
-        nc.gpsimd.tensor_tensor(tl_less_a[:], neg_a[:], tl_sb[:], ALU.add)
+        shifted_max = sb.tile([P, 1], F32, name="shifted_max")
+        nc.vector.tensor_scalar(shifted_max[:], neg_max[:], GUESS_SHIFT - 1.0, None, ALU.add)
         quantise(nc, htail_codes[:], htail_scales[:], htail_grouped[:])
 
-        log_sum = sb.tile([P, 1], F32, name="log_sum")
-        nc.scalar.activation(log_sum[:], row_sum[:], ACT.Ln)
-        neg_lse = sb.tile([P, 1], F32, name="neg_lse", tag="r_quarter1", align_bytes=64)
-        nc.scalar.activation(neg_lse[:], log_sum[:], ACT.Identity, bias=neg_max[:], scale=-1.0)
-        nc.scalar.activation(b[:, :U], tl_less_a[:], ACT.Identity, bias=neg_lse[:], scale=-1.0)
+        bits = row_sum[:].bitcast(U32)
+        small = {n: sb.tile([P, 1], F32, name=n) for n in ("e0", "ny", "nym", "sq", "e1", "sq1", "k")}
+        small["neg_lse"] = sb.tile([P, 1], F32, name="neg_lse", tag="lse_then_r", align_bytes=64)
+        nc.scalar.activation(small["e0"][:], bits, ACT.Exp, bias=GUESS_SHIFT, scale=-LN_PER_BIT)
+        nc.scalar.activation(small["ny"][:], bits, ACT.Identity, bias=GUESS_SHIFT - 0.5, scale=-LN_PER_BIT)
+        nc.scalar.activation(small["sq"][:], small["e0"][:], ACT.Square, bias=-2.0, scale=row_sum[:])
+        nc.scalar.activation(small["nym"][:], bits, ACT.Identity, bias=shifted_max[:], scale=-LN_PER_BIT)
+        nc.scalar.activation(small["e1"][:], small["sq"][:], ACT.Exp, bias=small["ny"][:], scale=0.5)
+        nc.scalar.activation(small["k"][:], small["sq"][:], ACT.Identity, bias=small["nym"][:], scale=0.5)
+        nc.scalar.activation(small["sq1"][:], small["e1"][:], ACT.Square, bias=-2.0, scale=row_sum[:])
+        nc.scalar.activation(small["neg_lse"][:], small["sq1"][:], ACT.Identity, bias=small["k"][:], scale=0.5)
+        log_p = sb.tile([P, U], F32, name="log_p")
+        nc.scalar.activation(log_p[:], a[:], ACT.Identity, bias=small["neg_lse"][:])
+        nc.gpsimd.tensor_tensor(b[:], log_p[:], tl_sb[:], ALU.subtract)
 
         listed_words = [sb.tile([P, HALF_I], U32, name="listed_words%d" % h, align_bytes=64) for h in range(2)]
         for h in range(2):
             entries = slice(h * HALF_I // 16, (h + 1) * HALF_I // 16)
             nc.vector.tensor_copy(listed_words[h][:], word_pool[:].indirect(word_list[:, entries]))
 
-        r_quarter0 = sb.tile([P, QUARTER_I], F32, name="r_quarter0")
-        r_quarter1 = sb.tile([P, QUARTER_I], F32, name="r_quarter1", tag="r_quarter1", align_bytes=64)
-        r_second = sb.tile([P, HALF_I], F32, name="r_second", tag="r_second", align_bytes=64)
-        r_sb = [r_quarter0[:], r_quarter1[:], r_second[:, :QUARTER_I], r_second[:, QUARTER_I:]]
+        r_sb = sb.tile([P, I], F32, name="r_sb", tag="lse_then_r", align_bytes=64)
         for first in range(0, I, QUARTER_I):
             h, start = divmod(first, HALF_I)
             bank = ps.tile([P, QUARTER_I], F32, name="r%d" % first)
@@ -149,11 +155,11 @@ def tile_attend_adaptivesoftmax_kernel(tc, hid, head, tl, htail, tail_words, tai
                 start=True,
                 stop=True,
             )
-            nc.scalar.copy(r_sb[first // QUARTER_I], bank[:])
+            nc.scalar.copy(r_sb[:, first : first + QUARTER_I], bank[:])
 
         for quarter, queue in enumerate((nc.sync, nc.sync, nc.scalar, nc.sync)):
             first, last = quarter * QUARTER_I, (quarter + 1) * QUARTER_I
             y = sb.tile([P, QUARTER_I], F32, name="y%d" % quarter)
             listed_b = b[:].indirect(cluster_list[:, first // 16 : last // 16])
-            nc.vector.tensor_tensor(y[:], listed_b, r_sb[quarter], ALU.add)
+            nc.vector.tensor_tensor(y[:], listed_b, r_sb[:, first:last], ALU.add)
             queue.dma_start(out=out[:, first:last], in_=y[:])

@@ -23,8 +23,10 @@ HALF_I = I // 2
 QUARTER_I = I // 4
 SCALE_ROW = P - 16
 SCALAR_U = 208
+PIECES = (256, 256, 352, 160)
 LN_PER_BIT = math.log(2.0) / 2**23
 GUESS_SHIFT = 88.0
+TERMS = 16
 
 
 def interleave(copy, grouped, raw):
@@ -60,7 +62,7 @@ def tile_attend_adaptivesoftmax_kernel(tc, hid, head, tl, htail, tail_words, tai
         nc.sync.dma_start(out=scale_pool[:].bitcast(I32)[SCALE_ROW:, :], in_=tail_scales[0].bitcast(I32))
         hid_raw = sb.tile([P, PACK, Q], F32, name="hid_raw")
         nc.sync.dma_start(out=hid_raw[:], in_=hid.rearrange("(p t) q -> p t q", t=PACK))
-        head_raw = sb.tile([P, PACK, U], F32, name="head_raw", tag="head_then_plane", align_bytes=64)
+        head_raw = sb.tile([P, PACK, U], F32, name="head_raw")
         nc.sync.dma_start(out=head_raw[:], in_=head.rearrange("(p t) u -> p t u", t=PACK))
         htail_raw = sb.tile([P, PACK, Q], F32, name="htail_raw")
         nc.sync.dma_start(out=htail_raw[:], in_=htail.rearrange("(p t) q -> p t q", t=PACK))
@@ -72,6 +74,12 @@ def tile_attend_adaptivesoftmax_kernel(tc, hid, head, tl, htail, tail_words, tai
         tl_sb = sb.tile([P, U], F32, name="tl_sb")
         nc.sync.dma_start(out=tl_sb[:], in_=tl)
         nc.sync.dma_start(cluster_list[:], offs2)
+
+        powers = sb.tile([P, TERMS], F32, name="powers")
+        nc.gpsimd.iota(powers[:], [[-1, TERMS]], base=TERMS, channel_multiplier=0, allow_small_or_imprecise_dtypes=True)
+        series = sb.tile([P, TERMS], F32, name="series")
+        nc.vector.reciprocal(series[:, : TERMS - 1], powers[:, 1:])
+        nc.vector.tensor_scalar(series[:, 0 : TERMS - 1 : 2], series[:, 0 : TERMS - 1 : 2], -1.0, None, ALU.mult)
 
         listed_scales = sb.tile([P, I], U8, name="listed_scales", align_bytes=64)
         nc.vector.tensor_copy(listed_scales[:], scale_pool[:].indirect(word_list[:]))
@@ -86,12 +94,14 @@ def tile_attend_adaptivesoftmax_kernel(tc, hid, head, tl, htail, tail_words, tai
         head_codes = sb.tile([P, U], U32, name="head_codes", align_bytes=64)
         head_scales = sb.tile([P, U], U8, name="head_scales", align_bytes=64)
         interleave(nc.scalar.copy, head_grouped[:, :SCALAR_U, :], head_raw[:, :, :SCALAR_U])
-        interleave(nc.vector.tensor_copy, head_grouped[:, SCALAR_U:, :], head_raw[:, :, SCALAR_U:])
-        a = ps.tile([P, U], F32, name="a")
-        for cols in (slice(U // 2, U), slice(0, U // 2)):
+        interleave(nc.vector.tensor_copy, head_grouped[:, U // 2 :, :], head_raw[:, :, U // 2 :])
+        interleave(nc.vector.tensor_copy, head_grouped[:, SCALAR_U : U // 2, :], head_raw[:, :, SCALAR_U : U // 2])
+        halves = (slice(U // 2, U), slice(0, U // 2))
+        a_banks = [ps.tile([P, U // 2], F32, name="a%d" % h) for h in range(2)]
+        for cols, bank in zip(halves, a_banks):
             quantise(nc, head_codes[:, cols], head_scales[:, cols], head_grouped[:, cols, :])
             nc.tensor.matmul_mx(
-                out=a[:, cols],
+                out=bank[:],
                 lhsT=hid_codes[:].bitcast(FP8X4),
                 lhsT_scale=hid_scales[:],
                 rhs=head_codes[:, cols].bitcast(FP8X4),
@@ -105,7 +115,7 @@ def tile_attend_adaptivesoftmax_kernel(tc, hid, head, tl, htail, tail_words, tai
         htail_scales = sb.tile([P, Q], U8, name="htail_scales", align_bytes=64)
         interleave(nc.scalar.copy, htail_grouped[:], htail_raw[:])
 
-        tail_plane = sb.tile([P, I], U8, name="tail_plane", tag="head_then_plane", align_bytes=64)
+        tail_plane = sb.tile([P, I], U8, name="tail_plane", align_bytes=64)
         nc.vector.memset(tail_plane[:].bitcast(I32), 0)
         for row in range(4):
             nc.scalar.dma_start(
@@ -113,28 +123,30 @@ def tile_attend_adaptivesoftmax_kernel(tc, hid, head, tl, htail, tail_words, tai
                 in_=listed_scales[:].bitcast(I32)[SCALE_ROW + row : P : 4, :],
             )
 
+        neg_a = sb.tile([P, U], F32, name="neg_a")
+        neg_max_half = sb.tile([P, 1], F32, name="neg_max_half")
         neg_max = sb.tile([P, 1], F32, name="neg_max")
-        nc.vector.tensor_reduce(neg_max[:], a[:], AXIS.X, ALU.max, negate=True)
+        nc.vector.tensor_scalar(neg_a[:, halves[0]], a_banks[0][:], -1.0, None, ALU.mult, ALU.min, accum_out=neg_max_half[:])
+        nc.vector.tensor_scalar(neg_a[:, halves[1]], a_banks[1][:], -1.0, neg_max_half[:], ALU.mult, ALU.min, accum_out=neg_max[:])
         p = sb.tile([P, U], F32, name="p")
         row_sum = sb.tile([P, 1], F32, name="row_sum")
-        nc.scalar.activation(p[:], a[:], ACT.Exp, bias=neg_max[:], accum_out=row_sum[:])
+        nc.scalar.activation(p[:], neg_a[:], ACT.Exp, bias=neg_max[:], scale=-1.0, accum_out=row_sum[:])
         shifted_max = sb.tile([P, 1], F32, name="shifted_max")
-        nc.vector.tensor_scalar(shifted_max[:], neg_max[:], GUESS_SHIFT - 1.0, None, ALU.add)
+        nc.vector.tensor_scalar(shifted_max[:], neg_max[:], GUESS_SHIFT, None, ALU.add)
         quantise(nc, htail_codes[:], htail_scales[:], htail_grouped[:])
 
         bits = row_sum[:].bitcast(U32)
-        small = {n: sb.tile([P, 1], F32, name=n) for n in ("e0", "ny", "nym", "sq", "e1", "sq1", "k")}
-        small["neg_lse"] = sb.tile([P, 1], F32, name="neg_lse", tag="lse_then_r", align_bytes=64)
-        nc.scalar.activation(small["e0"][:], bits, ACT.Exp, bias=GUESS_SHIFT, scale=-LN_PER_BIT)
-        nc.scalar.activation(small["ny"][:], bits, ACT.Identity, bias=GUESS_SHIFT - 0.5, scale=-LN_PER_BIT)
-        nc.scalar.activation(small["sq"][:], small["e0"][:], ACT.Square, bias=-2.0, scale=row_sum[:])
-        nc.scalar.activation(small["nym"][:], bits, ACT.Identity, bias=shifted_max[:], scale=-LN_PER_BIT)
-        nc.scalar.activation(small["e1"][:], small["sq"][:], ACT.Exp, bias=small["ny"][:], scale=0.5)
-        nc.scalar.activation(small["k"][:], small["sq"][:], ACT.Identity, bias=small["nym"][:], scale=0.5)
-        nc.scalar.activation(small["sq1"][:], small["e1"][:], ACT.Square, bias=-2.0, scale=row_sum[:])
-        nc.scalar.activation(small["neg_lse"][:], small["sq1"][:], ACT.Identity, bias=small["k"][:], scale=0.5)
+        inverse_guess = sb.tile([P, 1], F32, name="inverse_guess")
+        nc.scalar.activation(inverse_guess[:], bits, ACT.Exp, bias=GUESS_SHIFT, scale=-LN_PER_BIT)
+        nc.scalar.activation(series[:, TERMS - 1 : TERMS], bits, ACT.Identity, bias=shifted_max[:], scale=-LN_PER_BIT)
+        rest = sb.tile([P, 1], F32, name="rest")
+        nc.vector.tensor_scalar(rest[:], inverse_guess[:], row_sum[:], -1.0, ALU.mult, ALU.add)
+        horner = sb.tile([P, TERMS], F32, name="horner", tag="lse_then_r", align_bytes=64)
+        nc.vector.tensor_tensor_scan(
+            horner[:], rest[:].to_broadcast([P, TERMS]), series[:], 1.0 / TERMS, ALU.mult, ALU.add
+        )
         log_p = sb.tile([P, U], F32, name="log_p")
-        nc.scalar.activation(log_p[:], a[:], ACT.Identity, bias=small["neg_lse"][:])
+        nc.scalar.activation(log_p[:], neg_a[:], ACT.Identity, bias=horner[:, TERMS - 1 : TERMS], scale=-1.0)
         nc.gpsimd.tensor_tensor(b[:], log_p[:], tl_sb[:], ALU.subtract)
 
         listed_words = [sb.tile([P, HALF_I], U32, name="listed_words%d" % h, align_bytes=64) for h in range(2)]
@@ -157,9 +169,11 @@ def tile_attend_adaptivesoftmax_kernel(tc, hid, head, tl, htail, tail_words, tai
             )
             nc.scalar.copy(r_sb[:, first : first + QUARTER_I], bank[:])
 
-        for quarter, queue in enumerate((nc.sync, nc.sync, nc.scalar, nc.sync)):
-            first, last = quarter * QUARTER_I, (quarter + 1) * QUARTER_I
-            y = sb.tile([P, QUARTER_I], F32, name="y%d" % quarter)
+        first = 0
+        for piece, width in enumerate(PIECES):
+            last = first + width
+            y = sb.tile([P, width], F32, name="y%d" % piece)
             listed_b = b[:].indirect(cluster_list[:, first // 16 : last // 16])
             nc.vector.tensor_tensor(y[:], listed_b, r_sb[:, first:last], ALU.add)
-            queue.dma_start(out=out[:, first:last], in_=y[:])
+            nc.sync.dma_start(out=out[:, first:last], in_=y[:])
+            first = last

@@ -118,7 +118,7 @@ def tile_attend_adaptivesoftmax_kernel(tc, hid, head, tl, htail, tail_words, tai
         tail_plane = sb.tile([P, I], U8, name="tail_plane", align_bytes=64)
         nc.vector.memset(tail_plane[:].bitcast(I32), 0)
         for row in range(4):
-            nc.scalar.dma_start(
+            nc.sync.dma_start(
                 out=tail_plane[:].bitcast(I32)[row:P:32, :],
                 in_=listed_scales[:].bitcast(I32)[SCALE_ROW + row : P : 4, :],
             )

@@ -19,11 +19,11 @@ AXIS = mybir.AxisListType
 
 P = 128
 PACK = 4
-HALF_I = I // 2
 QUARTER_I = I // 4
 SCALE_ROW = P - 16
-SCALAR_U = 208
-PIECES = (256, 256, 352, 160)
+HALF_U = U // 2
+SCALAR_U = 96
+PIECES = (256, 256, 256, 128, 128)
 LN_PER_BIT = math.log(2.0) / 2**23
 GUESS_SHIFT = 88.0
 TERMS = 16
@@ -58,12 +58,18 @@ def tile_attend_adaptivesoftmax_kernel(tc, hid, head, tl, htail, tail_words, tai
         nc.vector.memset(scale_pool[:].bitcast(I32)[:SCALE_ROW, :], 0)
         b = sb.tile([P, U], F32, name="b")
 
-        nc.sync.dma_start(word_list[:], offs)
         nc.sync.dma_start(out=scale_pool[:].bitcast(I32)[SCALE_ROW:, :], in_=tail_scales[0].bitcast(I32))
+        nc.sync.dma_start(word_list[:], offs)
         hid_raw = sb.tile([P, PACK, Q], F32, name="hid_raw")
         nc.sync.dma_start(out=hid_raw[:], in_=hid.rearrange("(p t) q -> p t q", t=PACK))
-        head_raw = sb.tile([P, PACK, U], F32, name="head_raw")
-        nc.sync.dma_start(out=head_raw[:], in_=head.rearrange("(p t) u -> p t u", t=PACK))
+        head_rows = head.rearrange("(p t) u -> p t u", t=PACK)
+        halves = (slice(0, HALF_U), slice(HALF_U, U))
+        head_raw = [sb.tile([P, PACK, HALF_U], F32, name="head_raw%d" % h) for h in range(2)]
+        for h in range(2):
+            nc.sync.dma_start(out=head_raw[h][:], in_=head_rows[:, :, halves[h]])
+        tl_sb = sb.tile([P, U], F32, name="tl_sb")
+        nc.sync.dma_start(out=tl_sb[:], in_=tl)
+        nc.sync.dma_start(cluster_list[:], offs2)
         htail_raw = sb.tile([P, PACK, Q], F32, name="htail_raw")
         nc.sync.dma_start(out=htail_raw[:], in_=htail.rearrange("(p t) q -> p t q", t=PACK))
         word_pool = sb.tile([P, T], U32, name="word_pool", align_bytes=64)
@@ -71,9 +77,6 @@ def tile_attend_adaptivesoftmax_kernel(tc, hid, head, tl, htail, tail_words, tai
             out=word_pool[:].bitcast(I32),
             in_=tail_words[0].rearrange("p n t -> p (n t)").bitcast(I32),
         )
-        tl_sb = sb.tile([P, U], F32, name="tl_sb")
-        nc.sync.dma_start(out=tl_sb[:], in_=tl)
-        nc.sync.dma_start(cluster_list[:], offs2)
 
         powers = sb.tile([P, TERMS], F32, name="powers")
         nc.gpsimd.iota(powers[:], [[-1, TERMS]], base=TERMS, channel_multiplier=0, allow_small_or_imprecise_dtypes=True)
@@ -90,18 +93,18 @@ def tile_attend_adaptivesoftmax_kernel(tc, hid, head, tl, htail, tail_words, tai
         interleave(nc.scalar.copy, hid_grouped[:], hid_raw[:])
         quantise(nc, hid_codes[:], hid_scales[:], hid_grouped[:])
 
-        head_grouped = sb.tile([P, U, PACK], BF16, name="head_grouped", align_bytes=64)
+        head_grouped = [sb.tile([P, HALF_U, PACK], BF16, name="head_grouped%d" % h, align_bytes=64) for h in range(2)]
         head_codes = sb.tile([P, U], U32, name="head_codes", align_bytes=64)
         head_scales = sb.tile([P, U], U8, name="head_scales", align_bytes=64)
-        interleave(nc.scalar.copy, head_grouped[:, :SCALAR_U, :], head_raw[:, :, :SCALAR_U])
-        interleave(nc.vector.tensor_copy, head_grouped[:, U // 2 :, :], head_raw[:, :, U // 2 :])
-        interleave(nc.vector.tensor_copy, head_grouped[:, SCALAR_U : U // 2, :], head_raw[:, :, SCALAR_U : U // 2])
-        halves = (slice(U // 2, U), slice(0, U // 2))
-        a_banks = [ps.tile([P, U // 2], F32, name="a%d" % h) for h in range(2)]
-        for cols, bank in zip(halves, a_banks):
-            quantise(nc, head_codes[:, cols], head_scales[:, cols], head_grouped[:, cols, :])
+        interleave(nc.scalar.copy, head_grouped[0][:], head_raw[0][:])
+        interleave(nc.vector.tensor_copy, head_grouped[1][:, SCALAR_U:, :], head_raw[1][:, :, SCALAR_U:])
+        interleave(nc.scalar.copy, head_grouped[1][:, :SCALAR_U, :], head_raw[1][:, :, :SCALAR_U])
+        a_banks = [ps.tile([P, HALF_U], F32, name="a%d" % h) for h in range(2)]
+        for h in range(2):
+            cols = halves[h]
+            quantise(nc, head_codes[:, cols], head_scales[:, cols], head_grouped[h][:])
             nc.tensor.matmul_mx(
-                out=bank[:],
+                out=a_banks[h][:],
                 lhsT=hid_codes[:].bitcast(FP8X4),
                 lhsT_scale=hid_scales[:],
                 rhs=head_codes[:, cols].bitcast(FP8X4),
@@ -131,49 +134,50 @@ def tile_attend_adaptivesoftmax_kernel(tc, hid, head, tl, htail, tail_words, tai
         p = sb.tile([P, U], F32, name="p")
         row_sum = sb.tile([P, 1], F32, name="row_sum")
         nc.scalar.activation(p[:], neg_a[:], ACT.Exp, bias=neg_max[:], scale=-1.0, accum_out=row_sum[:])
+        tl_less_a = sb.tile([P, U], F32, name="tl_less_a")
+        nc.vector.tensor_tensor(tl_less_a[:], neg_a[:], tl_sb[:], ALU.add)
         shifted_max = sb.tile([P, 1], F32, name="shifted_max")
         nc.vector.tensor_scalar(shifted_max[:], neg_max[:], GUESS_SHIFT, None, ALU.add)
         quantise(nc, htail_codes[:], htail_scales[:], htail_grouped[:])
 
-        bits = row_sum[:].bitcast(U32)
         inverse_guess = sb.tile([P, 1], F32, name="inverse_guess")
-        nc.scalar.activation(inverse_guess[:], bits, ACT.Exp, bias=GUESS_SHIFT, scale=-LN_PER_BIT)
-        nc.scalar.activation(series[:, TERMS - 1 : TERMS], bits, ACT.Identity, bias=shifted_max[:], scale=-LN_PER_BIT)
+        nc.scalar.activation(inverse_guess[:], row_sum[:].bitcast(U32), ACT.Exp, bias=GUESS_SHIFT, scale=-LN_PER_BIT)
+        nc.vector.tensor_scalar(
+            series[:, TERMS - 1 : TERMS], row_sum[:].bitcast(I32), -LN_PER_BIT, shifted_max[:], ALU.mult, ALU.add
+        )
         rest = sb.tile([P, 1], F32, name="rest")
         nc.vector.tensor_scalar(rest[:], inverse_guess[:], row_sum[:], -1.0, ALU.mult, ALU.add)
-        horner = sb.tile([P, TERMS], F32, name="horner", tag="lse_then_r", align_bytes=64)
+        horner = sb.tile([P, TERMS], F32, name="horner")
         nc.vector.tensor_tensor_scan(
             horner[:], rest[:].to_broadcast([P, TERMS]), series[:], 1.0 / TERMS, ALU.mult, ALU.add
         )
-        log_p = sb.tile([P, U], F32, name="log_p")
-        nc.scalar.activation(log_p[:], neg_a[:], ACT.Identity, bias=horner[:, TERMS - 1 : TERMS], scale=-1.0)
-        nc.gpsimd.tensor_tensor(b[:], log_p[:], tl_sb[:], ALU.subtract)
+        nc.vector.tensor_scalar(b[:], tl_less_a[:], -1.0, horner[:, TERMS - 1 : TERMS], ALU.mult, ALU.add)
 
-        listed_words = [sb.tile([P, HALF_I], U32, name="listed_words%d" % h, align_bytes=64) for h in range(2)]
-        for h in range(2):
-            entries = slice(h * HALF_I // 16, (h + 1) * HALF_I // 16)
-            nc.vector.tensor_copy(listed_words[h][:], word_pool[:].indirect(word_list[:, entries]))
+        listed_b = [sb.tile([P, QUARTER_I], F32, name="listed_b%d" % j) for j in range(4)]
+        for j in range(4):
+            entries = slice(j * QUARTER_I // 16, (j + 1) * QUARTER_I // 16)
+            nc.scalar.activation(listed_b[j][:], b[:].indirect(cluster_list[:, entries]), ACT.Copy)
 
-        r_sb = sb.tile([P, I], F32, name="r_sb", tag="lse_then_r", align_bytes=64)
-        for first in range(0, I, QUARTER_I):
-            h, start = divmod(first, HALF_I)
-            bank = ps.tile([P, QUARTER_I], F32, name="r%d" % first)
+        listed_words = [sb.tile([P, QUARTER_I], U32, name="listed_words%d" % j, align_bytes=64) for j in range(4)]
+        for j in range(4):
+            entries = slice(j * QUARTER_I // 16, (j + 1) * QUARTER_I // 16)
+            nc.vector.tensor_copy(listed_words[j][:], word_pool[:].indirect(word_list[:, entries]))
+
+        first = 0
+        for width in PIECES:
+            last = first + width
+            j, start = divmod(first, QUARTER_I)
+            bank = ps.tile([P, width], F32, name="r%d" % first)
             nc.tensor.matmul_mx(
                 out=bank[:],
                 lhsT=htail_codes[:].bitcast(FP8X4),
                 lhsT_scale=htail_scales[:],
-                rhs=listed_words[h][:, start : start + QUARTER_I].bitcast(FP8X4),
-                rhs_scale=tail_plane[:, first : first + QUARTER_I],
+                rhs=listed_words[j][:, start : start + width].bitcast(FP8X4),
+                rhs_scale=tail_plane[:, first:last],
                 start=True,
                 stop=True,
             )
-            nc.scalar.copy(r_sb[:, first : first + QUARTER_I], bank[:])
-
-        first = 0
-        for piece, width in enumerate(PIECES):
-            last = first + width
-            y = sb.tile([P, width], F32, name="y%d" % piece)
-            listed_b = b[:].indirect(cluster_list[:, first // 16 : last // 16])
-            nc.vector.tensor_tensor(y[:], listed_b, r_sb[:, first:last], ALU.add)
+            y = sb.tile([P, width], F32, name="y%d" % first)
+            nc.vector.tensor_tensor(y[:], bank[:], listed_b[j][:, start : start + width], ALU.add)
             nc.sync.dma_start(out=out[:, first:last], in_=y[:])
             first = last

@@ -21,8 +21,7 @@ P = 128
 PACK = 4
 QUARTER_I = I // 4
 SCALE_ROW = P - 16
-HALF_U = U // 2
-SCALAR_U = 96
+SCALAR_U = 208
 PIECES = (256, 256, 256, 128, 128)
 LN_PER_BIT = math.log(2.0) / 2**23
 GUESS_SHIFT = 88.0
@@ -62,21 +61,18 @@ def tile_attend_adaptivesoftmax_kernel(tc, hid, head, tl, htail, tail_words, tai
         nc.sync.dma_start(word_list[:], offs)
         hid_raw = sb.tile([P, PACK, Q], F32, name="hid_raw")
         nc.sync.dma_start(out=hid_raw[:], in_=hid.rearrange("(p t) q -> p t q", t=PACK))
-        head_rows = head.rearrange("(p t) u -> p t u", t=PACK)
-        halves = (slice(0, HALF_U), slice(HALF_U, U))
-        head_raw = [sb.tile([P, PACK, HALF_U], F32, name="head_raw%d" % h) for h in range(2)]
-        for h in range(2):
-            nc.sync.dma_start(out=head_raw[h][:], in_=head_rows[:, :, halves[h]])
+        head_raw = sb.tile([P, PACK, U], F32, name="head_raw")
+        nc.sync.dma_start(out=head_raw[:], in_=head.rearrange("(p t) u -> p t u", t=PACK))
         tl_sb = sb.tile([P, U], F32, name="tl_sb")
         nc.sync.dma_start(out=tl_sb[:], in_=tl)
-        nc.sync.dma_start(cluster_list[:], offs2)
-        htail_raw = sb.tile([P, PACK, Q], F32, name="htail_raw")
-        nc.sync.dma_start(out=htail_raw[:], in_=htail.rearrange("(p t) q -> p t q", t=PACK))
         word_pool = sb.tile([P, T], U32, name="word_pool", align_bytes=64)
         nc.sync.dma_start(
             out=word_pool[:].bitcast(I32),
             in_=tail_words[0].rearrange("p n t -> p (n t)").bitcast(I32),
         )
+        htail_raw = sb.tile([P, PACK, Q], F32, name="htail_raw", tag="htail_then_words", align_bytes=64)
+        nc.sync.dma_start(out=htail_raw[:], in_=htail.rearrange("(p t) q -> p t q", t=PACK))
+        nc.sync.dma_start(cluster_list[:], offs2)
 
         powers = sb.tile([P, TERMS], F32, name="powers")
         nc.gpsimd.iota(powers[:], [[-1, TERMS]], base=TERMS, channel_multiplier=0, allow_small_or_imprecise_dtypes=True)
@@ -93,18 +89,18 @@ def tile_attend_adaptivesoftmax_kernel(tc, hid, head, tl, htail, tail_words, tai
         interleave(nc.scalar.copy, hid_grouped[:], hid_raw[:])
         quantise(nc, hid_codes[:], hid_scales[:], hid_grouped[:])
 
-        head_grouped = [sb.tile([P, HALF_U, PACK], BF16, name="head_grouped%d" % h, align_bytes=64) for h in range(2)]
+        head_grouped = sb.tile([P, U, PACK], BF16, name="head_grouped", align_bytes=64)
         head_codes = sb.tile([P, U], U32, name="head_codes", align_bytes=64)
         head_scales = sb.tile([P, U], U8, name="head_scales", align_bytes=64)
-        interleave(nc.scalar.copy, head_grouped[0][:], head_raw[0][:])
-        interleave(nc.vector.tensor_copy, head_grouped[1][:, SCALAR_U:, :], head_raw[1][:, :, SCALAR_U:])
-        interleave(nc.scalar.copy, head_grouped[1][:, :SCALAR_U, :], head_raw[1][:, :, :SCALAR_U])
-        a_banks = [ps.tile([P, HALF_U], F32, name="a%d" % h) for h in range(2)]
-        for h in range(2):
-            cols = halves[h]
-            quantise(nc, head_codes[:, cols], head_scales[:, cols], head_grouped[h][:])
+        interleave(nc.scalar.copy, head_grouped[:, :SCALAR_U, :], head_raw[:, :, :SCALAR_U])
+        interleave(nc.vector.tensor_copy, head_grouped[:, U // 2 :, :], head_raw[:, :, U // 2 :])
+        interleave(nc.vector.tensor_copy, head_grouped[:, SCALAR_U : U // 2, :], head_raw[:, :, SCALAR_U : U // 2])
+        halves = (slice(U // 2, U), slice(0, U // 2))
+        a_banks = [ps.tile([P, U // 2], F32, name="a%d" % h) for h in range(2)]
+        for cols, bank in zip(halves, a_banks):
+            quantise(nc, head_codes[:, cols], head_scales[:, cols], head_grouped[:, cols, :])
             nc.tensor.matmul_mx(
-                out=a_banks[h][:],
+                out=bank[:],
                 lhsT=hid_codes[:].bitcast(FP8X4),
                 lhsT_scale=hid_scales[:],
                 rhs=head_codes[:, cols].bitcast(FP8X4),
@@ -112,11 +108,6 @@ def tile_attend_adaptivesoftmax_kernel(tc, hid, head, tl, htail, tail_words, tai
                 start=True,
                 stop=True,
             )
-
-        htail_grouped = sb.tile([P, Q, PACK], BF16, name="htail_grouped", align_bytes=64)
-        htail_codes = sb.tile([P, Q], U32, name="htail_codes", align_bytes=64)
-        htail_scales = sb.tile([P, Q], U8, name="htail_scales", align_bytes=64)
-        interleave(nc.scalar.copy, htail_grouped[:], htail_raw[:])
 
         tail_plane = sb.tile([P, I], U8, name="tail_plane", align_bytes=64)
         nc.vector.memset(tail_plane[:].bitcast(I32), 0)
@@ -138,7 +129,6 @@ def tile_attend_adaptivesoftmax_kernel(tc, hid, head, tl, htail, tail_words, tai
         nc.vector.tensor_tensor(tl_less_a[:], neg_a[:], tl_sb[:], ALU.add)
         shifted_max = sb.tile([P, 1], F32, name="shifted_max")
         nc.vector.tensor_scalar(shifted_max[:], neg_max[:], GUESS_SHIFT, None, ALU.add)
-        quantise(nc, htail_codes[:], htail_scales[:], htail_grouped[:])
 
         inverse_guess = sb.tile([P, 1], F32, name="inverse_guess")
         nc.scalar.activation(inverse_guess[:], row_sum[:].bitcast(U32), ACT.Exp, bias=GUESS_SHIFT, scale=-LN_PER_BIT)
@@ -151,17 +141,33 @@ def tile_attend_adaptivesoftmax_kernel(tc, hid, head, tl, htail, tail_words, tai
         nc.vector.tensor_tensor_scan(
             horner[:], rest[:].to_broadcast([P, TERMS]), series[:], 1.0 / TERMS, ALU.mult, ALU.add
         )
-        nc.vector.tensor_scalar(b[:], tl_less_a[:], -1.0, horner[:, TERMS - 1 : TERMS], ALU.mult, ALU.add)
+        nc.scalar.activation(b[:], tl_less_a[:], ACT.Identity, bias=horner[:, TERMS - 1 : TERMS], scale=-1.0)
 
-        listed_b = [sb.tile([P, QUARTER_I], F32, name="listed_b%d" % j) for j in range(4)]
-        for j in range(4):
-            entries = slice(j * QUARTER_I // 16, (j + 1) * QUARTER_I // 16)
-            nc.scalar.activation(listed_b[j][:], b[:].indirect(cluster_list[:, entries]), ACT.Copy)
+        def entries(j):
+            return slice(j * QUARTER_I // 16, (j + 1) * QUARTER_I // 16)
 
-        listed_words = [sb.tile([P, QUARTER_I], U32, name="listed_words%d" % j, align_bytes=64) for j in range(4)]
-        for j in range(4):
-            entries = slice(j * QUARTER_I // 16, (j + 1) * QUARTER_I // 16)
-            nc.vector.tensor_copy(listed_words[j][:], word_pool[:].indirect(word_list[:, entries]))
+        def look_up(j, columns):
+            nc.scalar.activation(columns, b[:].indirect(cluster_list[:, entries(j)]), ACT.Copy)
+            return columns
+
+        def gather_words(j, columns):
+            nc.vector.tensor_copy(columns, word_pool[:].indirect(word_list[:, entries(j)]))
+            return columns
+
+        def quarter(tile, j):
+            return tile[:, j * QUARTER_I : (j + 1) * QUARTER_I]
+
+        looked_up = sb.tile([P, I], F32, name="looked_up")
+        listed_b = [look_up(j, quarter(looked_up, j)) for j in range(4)]
+        early_words = sb.tile([P, 2 * QUARTER_I], U32, name="early_words", align_bytes=64)
+        listed_words = [gather_words(j, quarter(early_words, j)) for j in range(2)]
+        htail_grouped = sb.tile([P, Q, PACK], BF16, name="htail_grouped", align_bytes=64)
+        htail_codes = sb.tile([P, Q], U32, name="htail_codes", align_bytes=64)
+        htail_scales = sb.tile([P, Q], U8, name="htail_scales", align_bytes=64)
+        nc.gpsimd.tensor_scalar(htail_grouped[:], htail_raw[:].rearrange("p t q -> p q t"), 1.0, 0.0, ALU.mult, ALU.add)
+        quantise(nc, htail_codes[:], htail_scales[:], htail_grouped[:])
+        late_words = sb.tile([P, 2 * QUARTER_I], U32, name="late_words", tag="htail_then_words", align_bytes=64)
+        listed_words = listed_words + [gather_words(2 + j, quarter(late_words, j)) for j in range(2)]
 
         first = 0
         for width in PIECES:

@@ -22,7 +22,7 @@ PACK = 4
 QUARTER_I = I // 4
 SCALE_ROW = P - 16
 SCALAR_U = 208
-PIECES = (256, 256, 256, 128, 128)
+PIECES = (256, 256, 256, 256)
 LN_PER_BIT = math.log(2.0) / 2**23
 GUESS_SHIFT = 88.0
 TERMS = 16
@@ -164,7 +164,7 @@ def tile_attend_adaptivesoftmax_kernel(tc, hid, head, tl, htail, tail_words, tai
         htail_grouped = sb.tile([P, Q, PACK], BF16, name="htail_grouped", align_bytes=64)
         htail_codes = sb.tile([P, Q], U32, name="htail_codes", align_bytes=64)
         htail_scales = sb.tile([P, Q], U8, name="htail_scales", align_bytes=64)
-        nc.gpsimd.tensor_scalar(htail_grouped[:], htail_raw[:].rearrange("p t q -> p q t"), 1.0, 0.0, ALU.mult, ALU.add)
+        interleave(nc.scalar.copy, htail_grouped[:], htail_raw[:])
         quantise(nc, htail_codes[:], htail_scales[:], htail_grouped[:])
         late_words = sb.tile([P, 2 * QUARTER_I], U32, name="late_words", tag="htail_then_words", align_bytes=64)
         listed_words = listed_words + [gather_words(2 + j, quarter(late_words, j)) for j in range(2)]

@@ -141,7 +141,7 @@ def tile_attend_adaptivesoftmax_kernel(tc, hid, head, tl, htail, tail_words, tai
         nc.vector.tensor_tensor_scan(
             horner[:], rest[:].to_broadcast([P, TERMS]), series[:], 1.0 / TERMS, ALU.mult, ALU.add
         )
-        nc.scalar.activation(b[:], tl_less_a[:], ACT.Identity, bias=horner[:, TERMS - 1 : TERMS], scale=-1.0)
+        nc.gpsimd.tensor_scalar(b[:], tl_less_a[:], -1.0, horner[:, TERMS - 1 : TERMS], ALU.mult, ALU.add)
 
         def entries(j):
             return slice(j * QUARTER_I // 16, (j + 1) * QUARTER_I // 16)

@@ -141,7 +141,9 @@ def tile_attend_adaptivesoftmax_kernel(tc, hid, head, tl, htail, tail_words, tai
         nc.vector.tensor_tensor_scan(
             horner[:], rest[:].to_broadcast([P, TERMS]), series[:], 1.0 / TERMS, ALU.mult, ALU.add
         )
-        nc.gpsimd.tensor_scalar(b[:], tl_less_a[:], -1.0, horner[:, TERMS - 1 : TERMS], ALU.mult, ALU.add)
+        neg_lse = horner[:, TERMS - 1 : TERMS]
+        nc.gpsimd.tensor_scalar(b[:, halves[0]], tl_less_a[:, halves[0]], -1.0, neg_lse, ALU.mult, ALU.add)
+        nc.scalar.activation(b[:, halves[1]], tl_less_a[:, halves[1]], ACT.Identity, bias=neg_lse, scale=-1.0)
 
         def entries(j):
             return slice(j * QUARTER_I // 16, (j + 1) * QUARTER_I // 16)
@@ -164,7 +166,10 @@ def tile_attend_adaptivesoftmax_kernel(tc, hid, head, tl, htail, tail_words, tai
         htail_grouped = sb.tile([P, Q, PACK], BF16, name="htail_grouped", align_bytes=64)
         htail_codes = sb.tile([P, Q], U32, name="htail_codes", align_bytes=64)
         htail_scales = sb.tile([P, Q], U8, name="htail_scales", align_bytes=64)
-        interleave(nc.scalar.copy, htail_grouped[:], htail_raw[:])
+        interleave(nc.scalar.copy, htail_grouped[:, : Q // 2, :], htail_raw[:, :, : Q // 2])
+        nc.gpsimd.tensor_scalar(
+            htail_grouped[:, Q // 2 :, :], htail_raw[:, :, Q // 2 :].rearrange("p t q -> p q t"), 1.0, 0.0, ALU.mult, ALU.add
+        )
         quantise(nc, htail_codes[:], htail_scales[:], htail_grouped[:])
         late_words = sb.tile([P, 2 * QUARTER_I], U32, name="late_words", tag="htail_then_words", align_bytes=64)
         listed_words = listed_words + [gather_words(2 + j, quarter(late_words, j)) for j in range(2)]

@@ -21,11 +21,12 @@ P = 128
 PACK = 4
 QUARTER_I = I // 4
 SCALE_ROW = P - 16
-SCALAR_U = 208
+SCALAR_SHARES = (64, 144)
 PIECES = (256, 256, 256, 256)
 LN_PER_BIT = math.log(2.0) / 2**23
 GUESS_SHIFT = 88.0
 TERMS = 16
+SCALAR_B = 384
 
 
 def interleave(copy, grouped, raw):
@@ -92,10 +93,11 @@ def tile_attend_adaptivesoftmax_kernel(tc, hid, head, tl, htail, tail_words, tai
         head_grouped = sb.tile([P, U, PACK], BF16, name="head_grouped", align_bytes=64)
         head_codes = sb.tile([P, U], U32, name="head_codes", align_bytes=64)
         head_scales = sb.tile([P, U], U8, name="head_scales", align_bytes=64)
-        interleave(nc.scalar.copy, head_grouped[:, :SCALAR_U, :], head_raw[:, :, :SCALAR_U])
-        interleave(nc.vector.tensor_copy, head_grouped[:, U // 2 :, :], head_raw[:, :, U // 2 :])
-        interleave(nc.vector.tensor_copy, head_grouped[:, SCALAR_U : U // 2, :], head_raw[:, :, SCALAR_U : U // 2])
         halves = (slice(U // 2, U), slice(0, U // 2))
+        for cols, share in zip(halves, SCALAR_SHARES):
+            middle = cols.start + share
+            interleave(nc.scalar.copy, head_grouped[:, cols.start : middle, :], head_raw[:, :, cols.start : middle])
+            interleave(nc.vector.tensor_copy, head_grouped[:, middle : cols.stop, :], head_raw[:, :, middle : cols.stop])
         a_banks = [ps.tile([P, U // 2], F32, name="a%d" % h) for h in range(2)]
         for cols, bank in zip(halves, a_banks):
             quantise(nc, head_codes[:, cols], head_scales[:, cols], head_grouped[:, cols, :])
@@ -142,8 +144,8 @@ def tile_attend_adaptivesoftmax_kernel(tc, hid, head, tl, htail, tail_words, tai
             horner[:], rest[:].to_broadcast([P, TERMS]), series[:], 1.0 / TERMS, ALU.mult, ALU.add
         )
         neg_lse = horner[:, TERMS - 1 : TERMS]
-        nc.gpsimd.tensor_scalar(b[:, halves[0]], tl_less_a[:, halves[0]], -1.0, neg_lse, ALU.mult, ALU.add)
-        nc.scalar.activation(b[:, halves[1]], tl_less_a[:, halves[1]], ACT.Identity, bias=neg_lse, scale=-1.0)
+        nc.gpsimd.tensor_scalar(b[:, SCALAR_B:], tl_less_a[:, SCALAR_B:], -1.0, neg_lse, ALU.mult, ALU.add)
+        nc.scalar.activation(b[:, :SCALAR_B], tl_less_a[:, :SCALAR_B], ACT.Identity, bias=neg_lse, scale=-1.0)
 
         def entries(j):
             return slice(j * QUARTER_I // 16, (j + 1) * QUARTER_I // 16)

@@ -15,14 +15,13 @@ U8 = mybir.dt.uint8
 FP8X4 = mybir.dt.float8_e4m3fn_x4
 ALU = mybir.AluOpType
 ACT = mybir.ActivationFunctionType
-AXIS = mybir.AxisListType
 
 P = 128
 PACK = 4
 QUARTER_I = I // 4
 SCALE_ROW = P - 16
 SCALAR_SHARES = (64, 144)
-PIECES = (256, 256, 256, 256)
+EARLY_WORDS = 640
 LN_PER_BIT = math.log(2.0) / 2**23
 GUESS_SHIFT = 88.0
 TERMS = 16
@@ -154,17 +153,13 @@ def tile_attend_adaptivesoftmax_kernel(tc, hid, head, tl, htail, tail_words, tai
             nc.scalar.activation(columns, b[:].indirect(cluster_list[:, entries(j)]), ACT.Copy)
             return columns
 
-        def gather_words(j, columns):
-            nc.vector.tensor_copy(columns, word_pool[:].indirect(word_list[:, entries(j)]))
-            return columns
-
         def quarter(tile, j):
             return tile[:, j * QUARTER_I : (j + 1) * QUARTER_I]
 
         looked_up = sb.tile([P, I], F32, name="looked_up")
         listed_b = [look_up(j, quarter(looked_up, j)) for j in range(4)]
-        early_words = sb.tile([P, 2 * QUARTER_I], U32, name="early_words", align_bytes=64)
-        listed_words = [gather_words(j, quarter(early_words, j)) for j in range(2)]
+        early_words = sb.tile([P, EARLY_WORDS], U32, name="early_words", align_bytes=64)
+        nc.vector.tensor_copy(early_words[:], word_pool[:].indirect(word_list[:, : EARLY_WORDS // 16]))
         htail_grouped = sb.tile([P, Q, PACK], BF16, name="htail_grouped", align_bytes=64)
         htail_codes = sb.tile([P, Q], U32, name="htail_codes", align_bytes=64)
         htail_scales = sb.tile([P, Q], U8, name="htail_scales", align_bytes=64)
@@ -173,24 +168,24 @@ def tile_attend_adaptivesoftmax_kernel(tc, hid, head, tl, htail, tail_words, tai
             htail_grouped[:, Q // 2 :, :], htail_raw[:, :, Q // 2 :].rearrange("p t q -> p q t"), 1.0, 0.0, ALU.mult, ALU.add
         )
         quantise(nc, htail_codes[:], htail_scales[:], htail_grouped[:])
-        late_words = sb.tile([P, 2 * QUARTER_I], U32, name="late_words", tag="htail_then_words", align_bytes=64)
-        listed_words = listed_words + [gather_words(2 + j, quarter(late_words, j)) for j in range(2)]
+        late_words = sb.tile([P, I - EARLY_WORDS], U32, name="late_words", tag="htail_then_words", align_bytes=64)
+        nc.vector.tensor_copy(late_words[:], word_pool[:].indirect(word_list[:, EARLY_WORDS // 16 :]))
 
-        first = 0
-        for width in PIECES:
-            last = first + width
-            j, start = divmod(first, QUARTER_I)
-            bank = ps.tile([P, width], F32, name="r%d" % first)
-            nc.tensor.matmul_mx(
-                out=bank[:],
-                lhsT=htail_codes[:].bitcast(FP8X4),
-                lhsT_scale=htail_scales[:],
-                rhs=listed_words[j][:, start : start + width].bitcast(FP8X4),
-                rhs_scale=tail_plane[:, first:last],
-                start=True,
-                stop=True,
-            )
-            y = sb.tile([P, width], F32, name="y%d" % first)
-            nc.vector.tensor_tensor(y[:], bank[:], listed_b[j][:, start : start + width], ALU.add)
+        for j in range(4):
+            first, last = j * QUARTER_I, (j + 1) * QUARTER_I
+            cuts = (first, EARLY_WORDS, last) if first < EARLY_WORDS < last else (first, last)
+            bank = ps.tile([P, QUARTER_I], F32, name="r%d" % j)
+            for start, stop in zip(cuts, cuts[1:]):
+                words = early_words[:, start:stop] if stop <= EARLY_WORDS else late_words[:, start - EARLY_WORDS : stop - EARLY_WORDS]
+                nc.tensor.matmul_mx(
+                    out=bank[:, start - first : stop - first],
+                    lhsT=htail_codes[:].bitcast(FP8X4),
+                    lhsT_scale=htail_scales[:],
+                    rhs=words.bitcast(FP8X4),
+                    rhs_scale=tail_plane[:, start:stop],
+                    start=True,
+                    stop=True,
+                )
+            y = sb.tile([P, QUARTER_I], F32, name="y%d" % j)
+            nc.vector.tensor_tensor(y[:], bank[:], listed_b[j], ALU.add)
             nc.sync.dma_start(out=out[:, first:last], in_=y[:])
-            first = last

import math
from contextlib import ExitStack

import concourse.mybir as mybir

D, K, T, I, U, Q = 512, 512, 4096, 1024, 512, 128
FLOPS = 2 * Q * D * U + 2 * Q * K * I

F32 = mybir.dt.float32
BF16 = mybir.dt.bfloat16
I32 = mybir.dt.int32
U32 = mybir.dt.uint32
U16 = mybir.dt.uint16
U8 = mybir.dt.uint8
FP8X4 = mybir.dt.float8_e4m3fn_x4
ALU = mybir.AluOpType
ACT = mybir.ActivationFunctionType

P = 128
PACK = 4
QUARTER_I = I // 4
SCALE_ROW = P - 16
SCALAR_SHARES = (64, 144)
EARLY_WORDS = 640
LN_PER_BIT = math.log(2.0) / 2**23
GUESS_SHIFT = 88.0
TERMS = 16
SCALAR_B = 384


def interleave(copy, grouped, raw):
    copy(
        grouped.rearrange("p (c i) t -> p c t i", i=4),
        raw.rearrange("p t (c i) -> p c t i", i=4),
    )


def quantise(nc, codes, scales, grouped):
    nc.vector.quantize_mx(
        out=codes.bitcast(FP8X4),
        scales=scales,
        in_=grouped.rearrange("p w t -> p (w t)"),
    )


def tile_attend_adaptivesoftmax_kernel(tc, hid, head, tl, htail, tail_words, tail_scales, offs, offs2, out):
    nc = tc.nc
    with ExitStack() as ctx:
        lists = ctx.enter_context(tc.tile_pool(name="lists", bufs=1))
        sb = ctx.enter_context(tc.tile_pool(name="sb", bufs=1))
        ps = ctx.enter_context(tc.psum_pool(name="ps", bufs=1))

        word_list = lists.tile([P, I // 16], U16, name="word_list")
        cluster_list = lists.tile([P, I // 16], U16, name="cluster_list")

        scale_pool = sb.tile([P, T], U8, name="scale_pool", align_bytes=64)
        nc.vector.memset(scale_pool[:].bitcast(I32)[:SCALE_ROW, :], 0)
        b = sb.tile([P, U], F32, name="b")

        nc.sync.dma_start(out=scale_pool[:].bitcast(I32)[SCALE_ROW:, :], in_=tail_scales[0].bitcast(I32))
        nc.sync.dma_start(word_list[:], offs)
        hid_raw = sb.tile([P, PACK, Q], F32, name="hid_raw")
        nc.sync.dma_start(out=hid_raw[:], in_=hid.rearrange("(p t) q -> p t q", t=PACK))
        head_raw = sb.tile([P, PACK, U], F32, name="head_raw")
        nc.sync.dma_start(out=head_raw[:], in_=head.rearrange("(p t) u -> p t u", t=PACK))
        tl_sb = sb.tile([P, U], F32, name="tl_sb")
        nc.sync.dma_start(out=tl_sb[:], in_=tl)
        word_pool = sb.tile([P, T], U32, name="word_pool", align_bytes=64)
        nc.sync.dma_start(
            out=word_pool[:].bitcast(I32),
            in_=tail_words[0].rearrange("p n t -> p (n t)").bitcast(I32),
        )
        htail_raw = sb.tile([P, PACK, Q], F32, name="htail_raw", tag="htail_then_words", align_bytes=64)
        nc.sync.dma_start(out=htail_raw[:], in_=htail.rearrange("(p t) q -> p t q", t=PACK))
        nc.sync.dma_start(cluster_list[:], offs2)

        powers = sb.tile([P, TERMS], F32, name="powers")
        nc.gpsimd.iota(powers[:], [[-1, TERMS]], base=TERMS, channel_multiplier=0, allow_small_or_imprecise_dtypes=True)
        series = sb.tile([P, TERMS], F32, name="series")
        nc.vector.reciprocal(series[:, : TERMS - 1], powers[:, 1:])
        nc.vector.tensor_scalar(series[:, 0 : TERMS - 1 : 2], series[:, 0 : TERMS - 1 : 2], -1.0, None, ALU.mult)

        listed_scales = sb.tile([P, I], U8, name="listed_scales", align_bytes=64)
        nc.vector.tensor_copy(listed_scales[:], scale_pool[:].indirect(word_list[:]))

        hid_grouped = sb.tile([P, Q, PACK], BF16, name="hid_grouped", align_bytes=64)
        hid_codes = sb.tile([P, Q], U32, name="hid_codes", align_bytes=64)
        hid_scales = sb.tile([P, Q], U8, name="hid_scales", align_bytes=64)
        interleave(nc.scalar.copy, hid_grouped[:], hid_raw[:])
        quantise(nc, hid_codes[:], hid_scales[:], hid_grouped[:])

        head_grouped = sb.tile([P, U, PACK], BF16, name="head_grouped", align_bytes=64)
        head_codes = sb.tile([P, U], U32, name="head_codes", align_bytes=64)
        head_scales = sb.tile([P, U], U8, name="head_scales", align_bytes=64)
        halves = (slice(U // 2, U), slice(0, U // 2))
        for cols, share in zip(halves, SCALAR_SHARES):
            middle = cols.start + share
            interleave(nc.scalar.copy, head_grouped[:, cols.start : middle, :], head_raw[:, :, cols.start : middle])
            interleave(nc.vector.tensor_copy, head_grouped[:, middle : cols.stop, :], head_raw[:, :, middle : cols.stop])
        a_banks = [ps.tile([P, U // 2], F32, name="a%d" % h) for h in range(2)]
        for cols, bank in zip(halves, a_banks):
            quantise(nc, head_codes[:, cols], head_scales[:, cols], head_grouped[:, cols, :])
            nc.tensor.matmul_mx(
                out=bank[:],
                lhsT=hid_codes[:].bitcast(FP8X4),
                lhsT_scale=hid_scales[:],
                rhs=head_codes[:, cols].bitcast(FP8X4),
                rhs_scale=head_scales[:, cols],
                start=True,
                stop=True,
            )

        tail_plane = sb.tile([P, I], U8, name="tail_plane", align_bytes=64)
        nc.vector.memset(tail_plane[:].bitcast(I32), 0)
        for row in range(4):
            nc.sync.dma_start(
                out=tail_plane[:].bitcast(I32)[row:P:32, :],
                in_=listed_scales[:].bitcast(I32)[SCALE_ROW + row : P : 4, :],
            )

        neg_a = sb.tile([P, U], F32, name="neg_a")
        neg_max_half = sb.tile([P, 1], F32, name="neg_max_half")
        neg_max = sb.tile([P, 1], F32, name="neg_max")
        nc.vector.tensor_scalar(neg_a[:, halves[0]], a_banks[0][:], -1.0, None, ALU.mult, ALU.min, accum_out=neg_max_half[:])
        nc.vector.tensor_scalar(neg_a[:, halves[1]], a_banks[1][:], -1.0, neg_max_half[:], ALU.mult, ALU.min, accum_out=neg_max[:])
        p = sb.tile([P, U], F32, name="p")
        row_sum = sb.tile([P, 1], F32, name="row_sum")
        nc.scalar.activation(p[:], neg_a[:], ACT.Exp, bias=neg_max[:], scale=-1.0, accum_out=row_sum[:])
        tl_less_a = sb.tile([P, U], F32, name="tl_less_a")
        nc.vector.tensor_tensor(tl_less_a[:], neg_a[:], tl_sb[:], ALU.add)
        shifted_max = sb.tile([P, 1], F32, name="shifted_max")
        nc.vector.tensor_scalar(shifted_max[:], neg_max[:], GUESS_SHIFT, None, ALU.add)

        inverse_guess = sb.tile([P, 1], F32, name="inverse_guess")
        nc.scalar.activation(inverse_guess[:], row_sum[:].bitcast(U32), ACT.Exp, bias=GUESS_SHIFT, scale=-LN_PER_BIT)
        nc.vector.tensor_scalar(
            series[:, TERMS - 1 : TERMS], row_sum[:].bitcast(I32), -LN_PER_BIT, shifted_max[:], ALU.mult, ALU.add
        )
        rest = sb.tile([P, 1], F32, name="rest")
        nc.vector.tensor_scalar(rest[:], inverse_guess[:], row_sum[:], -1.0, ALU.mult, ALU.add)
        horner = sb.tile([P, TERMS], F32, name="horner")
        nc.vector.tensor_tensor_scan(
            horner[:], rest[:].to_broadcast([P, TERMS]), series[:], 1.0 / TERMS, ALU.mult, ALU.add
        )
        neg_lse = horner[:, TERMS - 1 : TERMS]
        nc.gpsimd.tensor_scalar(b[:, SCALAR_B:], tl_less_a[:, SCALAR_B:], -1.0, neg_lse, ALU.mult, ALU.add)
        nc.scalar.activation(b[:, :SCALAR_B], tl_less_a[:, :SCALAR_B], ACT.Identity, bias=neg_lse, scale=-1.0)

        def entries(j):
            return slice(j * QUARTER_I // 16, (j + 1) * QUARTER_I // 16)

        def look_up(j, columns):
            nc.scalar.activation(columns, b[:].indirect(cluster_list[:, entries(j)]), ACT.Copy)
            return columns

        def quarter(tile, j):
            return tile[:, j * QUARTER_I : (j + 1) * QUARTER_I]

        looked_up = sb.tile([P, I], F32, name="looked_up")
        listed_b = [look_up(j, quarter(looked_up, j)) for j in range(4)]
        early_words = sb.tile([P, EARLY_WORDS], U32, name="early_words", align_bytes=64)
        nc.vector.tensor_copy(early_words[:], word_pool[:].indirect(word_list[:, : EARLY_WORDS // 16]))
        htail_grouped = sb.tile([P, Q, PACK], BF16, name="htail_grouped", align_bytes=64)
        htail_codes = sb.tile([P, Q], U32, name="htail_codes", align_bytes=64)
        htail_scales = sb.tile([P, Q], U8, name="htail_scales", align_bytes=64)
        interleave(nc.scalar.copy, htail_grouped[:, : Q // 2, :], htail_raw[:, :, : Q // 2])
        nc.gpsimd.tensor_scalar(
            htail_grouped[:, Q // 2 :, :], htail_raw[:, :, Q // 2 :].rearrange("p t q -> p q t"), 1.0, 0.0, ALU.mult, ALU.add
        )
        quantise(nc, htail_codes[:], htail_scales[:], htail_grouped[:])
        late_words = sb.tile([P, I - EARLY_WORDS], U32, name="late_words", tag="htail_then_words", align_bytes=64)
        nc.vector.tensor_copy(late_words[:], word_pool[:].indirect(word_list[:, EARLY_WORDS // 16 :]))

        for j in range(4):
            first, last = j * QUARTER_I, (j + 1) * QUARTER_I
            cuts = (first, EARLY_WORDS, last) if first < EARLY_WORDS < last else (first, last)
            bank = ps.tile([P, QUARTER_I], F32, name="r%d" % j)
            for start, stop in zip(cuts, cuts[1:]):
                words = early_words[:, start:stop] if stop <= EARLY_WORDS else late_words[:, start - EARLY_WORDS : stop - EARLY_WORDS]
                nc.tensor.matmul_mx(
                    out=bank[:, start - first : stop - first],
                    lhsT=htail_codes[:].bitcast(FP8X4),
                    lhsT_scale=htail_scales[:],
                    rhs=words.bitcast(FP8X4),
                    rhs_scale=tail_plane[:, start:stop],
                    start=True,
                    stop=True,
                )
            y = sb.tile([P, QUARTER_I], F32, name="y%d" % j)
            nc.vector.tensor_tensor(y[:], bank[:], listed_b[j], ALU.add)
            nc.sync.dma_start(out=out[:, first:last], in_=y[:])
